import numpy as np
import ml_dtypes


def mxq(x, axis, fmt="e4m3"):
    dtype, down = {"e4m3": (ml_dtypes.float8_e4m3fn, 7), "e5m2": (ml_dtypes.float8_e5m2, 14)}[fmt]
    v = np.moveaxis(np.asarray(x, np.float32).astype(ml_dtypes.bfloat16).astype(np.float64), axis, -1)
    blocks = v.reshape(v.shape[:-1] + (-1, 32))
    amax = np.abs(blocks).max(-1, keepdims=True)
    byte = np.maximum(np.where(amax > 0, np.frexp(amax)[1] - 1 + 127, 0) - down, 1)
    scale = np.exp2(byte - 127.0)
    codes = (blocks / scale).astype(np.float32).astype(dtype).astype(np.float64)
    return np.moveaxis((codes * scale).reshape(v.shape), -1, axis)


WIDE = False


def mx_kscale(k):
    if not WIDE:
        return np.ones(k)
    levels = np.array([10, -10, 5, -5, 0])
    if k % 512:
        return np.exp2(np.random.permutation(np.resize(levels, k // 32))).repeat(32)
    a = np.empty((k // 512, 16))
    for p in range(k // 512):
        a[p, :8] = np.random.permutation(np.resize(levels, 8))
        for g in range(8):
            far = levels[np.abs(levels - a[p, g]) >= 10]
            a[p, g + 8] = far[np.random.randint(len(far))]
    return np.exp2(a.ravel()).repeat(32)


BF16 = ml_dtypes.bfloat16


def bf(x):
    return np.asarray(x, np.float32).astype(BF16)


def f64(x):
    return np.asarray(x).astype(np.float64)


E2M1 = np.array([0.0, 0.5, 1.0, 1.5, 2.0, 3.0, 4.0, 6.0, -0.0, -0.5, -1.0, -1.5, -2.0, -3.0, -4.0, -6.0])


def pack_weight(w, fmt):
    k, n = w.shape
    w = f64(bf(w)).reshape(k // 32, 32, n)
    amax = np.abs(w).max(1)
    if fmt == "e4m3":
        byte = np.frexp(amax)[1] - 1 + 127 - 7
    else:
        mant, ex = np.frexp(amax / 6.0)
        byte = np.where(mant > 0.5, ex, ex - 1) + 127
    byte = np.clip(np.where(amax > 0, byte, 1), 1, 254)
    scaled = (w * np.exp2(127.0 - byte)[:, None, :]).reshape(k, n).astype(np.float32)
    by_word = np.ascontiguousarray(scaled.reshape(k // 512, 128, 4, n).transpose(0, 1, 3, 2))
    if fmt == "e4m3":
        words = by_word.astype(ml_dtypes.float8_e4m3fn).view(np.uint8)
    else:
        c = by_word.astype(ml_dtypes.float4_e2m1fn).view(np.uint8) & 0xF
        words = c[..., 0::2] | (c[..., 1::2] << 4)
    return np.ascontiguousarray(words), np.ascontiguousarray(byte.astype(np.uint8).reshape(k // 512, 16, n))


def unpack_weight(words, scales, fmt):
    g, p, n, _ = words.shape
    if fmt == "e4m3":
        vals = np.ascontiguousarray(words).view(ml_dtypes.float8_e4m3fn).astype(np.float64)
    else:
        nib = np.empty((g, p, n, 4), np.uint8)
        nib[..., 0::2] = words & 0xF
        nib[..., 1::2] = words >> 4
        vals = E2M1[nib]
    vals = vals * np.repeat(np.exp2(scales.astype(np.float64) - 127.0), 8, axis=1)[..., None]
    return vals.transpose(0, 1, 3, 2).reshape(g * 512, n)
def pack4(w):
    words, scales = pack_weight(w, "e2m1")
    return words.reshape(words.shape[0], 128, -1), scales


def unpack4(words, scales):
    return unpack_weight(words.reshape(words.shape[0], 128, -1, 2), scales, "e2m1")


E4M3FN = np.array([(-1.0 if i & 128 else 1.0) * ((1.0 + (i & 7) / 8.0) * 2.0 ** (((i >> 3) & 15) - 7) if i & 120 else (i & 7) * 2.0 ** -9) for i in range(256)])


def e4m3fn_bytes(y):
    return np.clip(np.asarray(y, np.float64), -448.0, 448.0).astype(np.float32).astype(ml_dtypes.float8_e4m3fn).view(np.uint8)


def e4m3fn_values(b):
    return E4M3FN[b]


N, D, H, O, P = 1024, 1024, 1024, 1024, 2


def sigmoid(v):
    return 1.0 / (1.0 + np.exp(-v))


def jacobi_degree_one(u, alpha, beta):
    return (alpha + 1.0) + (alpha + beta + 2.0) * u


def jacobi_degree_two(u, alpha, beta):
    c0 = (alpha + 1.0) * (alpha + 2.0) / 2.0
    c1 = (alpha + 2.0) * (alpha + beta + 3.0)
    c2 = (alpha + beta + 3.0) * (alpha + beta + 4.0) / 2.0
    return c0 + c1 * u + c2 * (u * u)


def draw0():
    s = mx_kscale(D)
    t = np.stack([mx_kscale(H) for _ in range(P)])
    x = bf(np.random.standard_normal((N, D)) * s)
    w1_words, w1_scales = pack4(np.random.standard_normal((D, H)) * 1.5 / np.sqrt(D) / s[:, None])
    return {
        "x": x,
        "w1_words": w1_words,
        "w1_scales": w1_scales,
        "gamma": bf(np.random.uniform(0.6, 1.6, H)),
        "alpha": bf(np.random.uniform(0.0, 1.0, H)),
        "beta": bf(np.random.uniform(0.0, 1.0, H)),
        "g": bf((1.0 + 0.1 * np.random.standard_normal((P, H))) * t),
        "w2": bf(np.random.standard_normal((P, H, O)) / np.sqrt(H) / t[:, :, None]),
    }


def core(x, w1_words, w1_scales, gamma, alpha, beta, g, w2):
    z = mxq(f64(x), 1, "e4m3") @ unpack4(w1_words, w1_scales)

    u = np.power(sigmoid(z), f64(gamma)[None, :]) - 1.0

    a = f64(alpha)[None, :]
    b = f64(beta)[None, :]
    p1 = jacobi_degree_one(u, a, b)
    p2 = jacobi_degree_two(u, a, b)

    gain = f64(g)
    r1 = p1 * gain[0][None, :]
    r2 = p2 * gain[1][None, :]

    w = f64(w2)
    y1 = mxq(r1, 1, "e4m3") @ mxq(w[0], 0, "e4m3")
    y2 = mxq(r2, 1, "e4m3") @ mxq(w[1], 0, "e4m3")
    return y1 + y2


def setup_inputs():
    drawn = draw0()
    full = np.asarray(drawn['x']).astype(np.float64)
    scale = (np.abs(full).reshape(1024, 8, 128).max(axis=(2,)) / 448.0).astype(np.float32)
    given = {}
    for key, value in drawn.items():
        if key == 'x':
            given['x_bytes'] = e4m3fn_bytes(full / np.repeat(scale.astype(np.float64), 128, axis=1))
            given['x_scale'] = scale
        else:
            given[key] = value
    return given


def reference(x_bytes, x_scale, w1_words, w1_scales, gamma, alpha, beta, g, w2):
    return core(e4m3fn_values(x_bytes) * np.repeat(x_scale.astype(np.float64), 128, axis=1), w1_words, w1_scales, gamma, alpha, beta, g, w2)

@@ -1,0 +1,336 @@
+from contextlib import ExitStack
+
+import concourse.mybir as mybir
+from concourse.masks import make_identity
+
+N, D, H, O = 1024, 1024, 1024, 1024
+FLOPS = 2 * N * D * H + 2 * 2 * N * H * O
+
+F32 = mybir.dt.float32
+BF16 = mybir.dt.bfloat16
+I32 = mybir.dt.int32
+U32 = mybir.dt.uint32
+U8 = mybir.dt.uint8
+FP8 = mybir.dt.float8_e4m3fn
+FP8X4 = mybir.dt.float8_e4m3fn_x4
+FP4X4 = mybir.dt.float4_e2m1fn_x4
+ACT = mybir.ActivationFunctionType
+ALU = mybir.AluOpType
+
+P = 128
+TILES = 8
+CHUNK = 256
+STEPS = 8
+LN_FLOOR = 2.0 ** -64
+
+
+def tile_fractionaljacobikantwodegree_d1p_kernel(
+    tc, x_bytes, x_scale, w1_words, w1_scales, gamma, alpha, beta, g, w2, out
+):
+    nc = tc.nc
+    with ExitStack() as ctx:
+        sb = ctx.enter_context(tc.tile_pool(name="sb", bufs=1))
+        ps = ctx.enter_context(tc.psum_pool(name="ps", bufs=1))
+
+        def tiles(name, count, shape, dtype):
+            return [sb.tile(shape, dtype, name="%s%d" % (name, i), align_bytes=64) for i in range(count)]
+
+        bank = [ps.tile([P, 512], F32, name="bank%d" % i) for i in range(8)]
+
+        xb = tiles("xbytes", 2, [P, 2 * D], U8) + tiles("xbytes_late", 1, [P, 4 * D], U8)
+        xs = tiles("xscale", 1, [P, TILES * 8], F32)[0]
+        xw = tiles("xwide", 4, [P, D], BF16)
+        xg = tiles("xgrouped", 2, [P, 2, 2048], BF16)
+        xq = tiles("xcodes", 2, [P, 2, 512], U32)
+        xqs = tiles("xplane", 2, [P, 2, 512], U8)
+        w1r = tiles("w1raw", 1, [P, 2, 2 * H], U8)[0]
+        w1p = tiles("w1perm", 1, [P, 2, 2 * H], U8)[0]
+        s1r = tiles("s1raw", 1, [P, 2, H], U8)[0]
+        s1p = tiles("s1perm", 1, [P, 2, H], U8)[0]
+        ident = tiles("ident", 1, [P, P], F32)[0]
+        crow = tiles("crow", 1, [16, 512], BF16)[0]
+        cperm = tiles("cperm", 1, [P, 512], F32)[0]
+        coef = tiles("coef", 1, [P, 4, 16], F32)[0]
+        cw = tiles("cwork", 10, [P, 4, 2], F32)
+        warm = tiles("warm", 2, [P, 8], F32)
+        sig = tiles("sig", 1, [P, TILES, N], F32)[0]
+        w2r = tiles("w2raw", 4, [P, 4, O], BF16)
+        w2i = tiles("w2grouped", 2, [P, 2048], BF16)
+        w2q = tiles("w2codes", 4, [P, O], U32)
+        w2s = tiles("w2plane", 4, [P, O], U8)
+        sp = tiles("spow", 4, [P, 4, CHUNK], F32)
+        sq = tiles("ssq", 4, [P, 4, CHUNK], F32)
+        rp = tiles("rplanar", 2, [P, 4, 2 * CHUNK], BF16)
+        ri = tiles("rgrouped", 2, [P, 2048], BF16)
+        rq = tiles("rcodes", 3, [P, 2 * CHUNK], U32)
+        rs = tiles("rplane", 3, [P, 2 * CHUNK], U8)
+        ob = tiles("obuf", 8, [P, 512], F32)
+
+        ctx.enter_context(tc.manual_schedule())
+
+        xv = x_bytes.rearrange("(p j) k -> p (j k)", j=TILES)
+        outv = out.rearrange("(p j) o -> j p o", j=TILES)
+
+        def xbytes_of(j):
+            if j < 4:
+                return xb[j // 2][:, (j % 2) * D : (j % 2 + 1) * D]
+            return xb[2][:, (j - 4) * D : (j - 3) * D]
+
+        nc.vector.memset(warm[0][:], 0.0)
+        nc.vector.memset(s1r[:].rearrange("p g n -> p (g n)").bitcast(I32), 0)
+        nc.vector.memset(cperm[:], 0.0)
+        nc.scalar.activation(out=warm[1][:], in_=warm[0][:], func=ACT.Sigmoid)
+        make_identity(nc, ident[:])
+
+        nc.sync.dma_start(out=xs[:], in_=x_scale.rearrange("(p j) b -> p (j b)", j=TILES))
+        nc.sync.dma_start(out=xb[0][:, 0 : 2 * D], in_=xv[:, 0 : 2 * D])
+        nc.sync.dma_start(out=xb[1][:, 0 : 2 * D], in_=xv[:, 2 * D : 4 * D])
+        s1v = w1_scales.rearrange("g (a r) n -> r a g n", r=4)
+        for r in range(4):
+            nc.sync.dma_start(out=s1r[r:P:32].bitcast(I32), in_=s1v[r].bitcast(I32))
+        nc.sync.dma_start(out=w1r[:].bitcast(I32), in_=w1_words.rearrange("g p n -> p g n").bitcast(I32))
+        nc.sync.dma_start(out=xb[2][:], in_=xv[:, 4 * D : 8 * D])
+        nc.sync.dma_start(out=crow[0:2, :], in_=gamma.rearrange("(a n) -> a n", a=2))
+        nc.sync.dma_start(out=crow[2:4, :], in_=alpha.rearrange("(a n) -> a n", a=2))
+        nc.sync.dma_start(out=crow[4:6, :], in_=beta.rearrange("(a n) -> a n", a=2))
+        nc.sync.dma_start(out=crow[6:10, :], in_=g.rearrange("m (a n) -> (m a) n", a=2))
+        w2v = w2.rearrange("m (a q t e) o -> a m e q t o", a=2, t=4, e=4)
+        for a in range(2):
+            for m in range(2):
+                for e in range(4):
+                    nc.sync.dma_start(out=w2r[2 * a + m][e:P:4], in_=w2v[a, m, e])
+
+        def widen(j, on_scalar):
+            src = xbytes_of(j)
+            for b in range(8):
+                cols = slice(128 * b, 128 * (b + 1))
+                sc = xs[:, 8 * j + b : 8 * j + b + 1]
+                if on_scalar:
+                    nc.scalar.activation(out=xw[j % 4][:, cols], in_=src[:, cols].bitcast(FP8), func=ACT.Copy, scale=sc)
+                else:
+                    nc.vector.tensor_scalar(
+                        out=xw[j % 4][:, cols], in0=src[:, cols].bitcast(FP8), scalar1=sc, scalar2=None, op0=ALU.mult
+                    )
+
+        def turn(j):
+            words = xw[j % 4][:].bitcast(F32)
+            for a in range(2):
+                for u in range(2):
+                    i = 2 * a + u
+                    nc.tensor.transpose(
+                        bank[j % 4][:, 128 * i : 128 * (i + 1)], words[:, 256 * a + u : 256 * (a + 1) : 2], ident[:]
+                    )
+
+        def unload(j, on_scalar):
+            dst = xg[j // 4][:].bitcast(F32)[:, :, 256 * (j % 4) : 256 * (j % 4 + 1)].rearrange("p a (r u) -> p a r u", u=2)
+            src = bank[j % 4][:].rearrange("p (a u r) -> p a r u", a=2, u=2)
+            if on_scalar:
+                nc.scalar.copy(out=dst, in_=src)
+            else:
+                nc.vector.tensor_copy(out=dst, in_=src)
+
+        def quant_x(pair):
+            h, c = divmod(pair, 2)
+            for a in range(2):
+                nc.vector.quantize_mx(
+                    out=xq[h][:, a, 256 * c : 256 * (c + 1)].bitcast(FP8X4),
+                    scales=xqs[h][:, a, 256 * c : 256 * (c + 1)],
+                    in_=xg[h][:, a, 1024 * c : 1024 * (c + 1)],
+                )
+
+        def permute_w1():
+            for a in range(2):
+                nc.vector.tensor_copy(
+                    out=s1p[:, a, :].bitcast(I32).rearrange("p (b t q) -> p b t q", b=2, t=4),
+                    in_=s1r[:, a, :].bitcast(I32).rearrange("p (b q t) -> p b t q", b=2, t=4),
+                )
+                for b in range(2):
+                    cols = slice(1024 * b, 1024 * (b + 1))
+                    nc.vector.tensor_copy(
+                        out=w1p[:, a, cols].bitcast(I32).rearrange("p (t q w) -> p t q w", t=4, w=2),
+                        in_=w1r[:, a, cols].bitcast(I32).rearrange("p (q t w) -> p t q w", t=4, w=2),
+                    )
+
+        def project(h, i):
+            z = bank[4 + i % 4]
+            for a in range(2):
+                nc.tensor.matmul_mx(
+                    out=z[:],
+                    lhsT=w1p[:, a, 256 * i : 256 * (i + 1)].bitcast(FP4X4),
+                    lhsT_scale=s1p[:, a, 128 * i : 128 * (i + 1)],
+                    rhs=xq[h][:, a, :].bitcast(FP8X4),
+                    rhs_scale=xqs[h][:, a, :],
+                    start=(a == 0),
+                    stop=(a == 1),
+                )
+            nc.scalar.activation(out=sig[:, i, 512 * h : 512 * (h + 1)], in_=z[:], func=ACT.Sigmoid)
+
+        def interleave(dst, src):
+            nc.vector.tensor_copy(
+                out=dst.rearrange("p (c i t) -> p c t i", i=4, t=4), in_=src.rearrange("p t (c i) -> p c t i", i=4)
+            )
+
+        def w2_group(u):
+            interleave(w2i[u % 2][:], w2r[u // 2][:, :, 512 * (u % 2) : 512 * (u % 2 + 1)])
+
+        def w2_quant(u):
+            cols = slice(512 * (u % 2), 512 * (u % 2 + 1))
+            nc.vector.quantize_mx(out=w2q[u // 2][:, cols].bitcast(FP8X4), scales=w2s[u // 2][:, cols], in_=w2i[u % 2][:])
+
+        widen(0, False)
+        widen(1, True)
+        turn(0)
+        widen(2, False)
+        turn(1)
+        unload(0, True)
+        widen(3, False)
+        turn(2)
+        unload(1, True)
+        turn(3)
+        unload(2, True)
+        permute_w1()
+        quant_x(0)
+        unload(3, True)
+        widen(4, False)
+        quant_x(1)
+        widen(5, True)
+        widen(6, False)
+        widen(7, False)
+        for i in range(4):
+            project(0, i)
+        turn(4)
+        turn(5)
+        unload(4, False)
+        unload(5, False)
+        project(0, 4)
+        project(0, 5)
+        turn(6)
+        turn(7)
+        unload(6, False)
+        quant_x(2)
+        unload(7, False)
+        nc.vector.tensor_copy(
+            out=cperm[0:10, :].rearrange("p (t q e) -> p t q e", t=4, e=4),
+            in_=crow[0:10, :].rearrange("p (q t e) -> p t q e", t=4, e=4),
+        )
+        quant_x(3)
+        project(0, 6)
+        project(0, 7)
+        for t in range(4):
+            nc.tensor.transpose(bank[0][:, 128 * t : 128 * (t + 1)], cperm[:, 128 * t : 128 * (t + 1)], ident[:])
+        for i in range(TILES):
+            project(1, i)
+
+        gam, al, be, g0, g1 = [coef[:, :, 2 * v : 2 * v + 2] for v in range(5)]
+        ab, slope1, off1, ab4, inv, shift, c2h, slope2, eh, off2 = [c[:] for c in cw]
+
+        def stt(o, a, s, b, op0):
+            nc.vector.scalar_tensor_tensor(out=o, in0=a, scalar=s, in1=b, op0=op0, op1=ALU.mult)
+
+        small = [
+            lambda: nc.vector.tensor_copy(
+                out=coef[:], in_=bank[0][:].rearrange("p (t r) -> p t r", t=4)[:, :, 0:16]
+            ),
+            lambda: nc.vector.tensor_tensor(out=ab, in0=al, in1=be, op=ALU.add),
+            lambda: stt(off1, be, 1.0, g0, ALU.add),
+            lambda: nc.vector.tensor_scalar(out=ab4, in0=ab, scalar1=4.0, scalar2=None, op0=ALU.add),
+            lambda: stt(slope1, ab, 2.0, g0, ALU.add),
+            lambda: nc.vector.reciprocal(out=inv, in_=ab4),
+            lambda: stt(c2h, ab, 3.0, ab4, ALU.add),
+            lambda: stt(shift, be, 2.0, inv, ALU.add),
+            lambda: stt(slope2, c2h, 0.5, g1, ALU.mult),
+            lambda: stt(eh, al, 2.0, shift, ALU.add),
+            lambda: stt(off2, eh, 0.5, g1, ALU.mult),
+        ]
+        w2_group(0)
+        small[0]()
+        for u in range(1, 8):
+            w2_group(u)
+            if u <= 5:
+                small[2 * u - 1]()
+            w2_quant(u - 1)
+            if u <= 5:
+                small[2 * u]()
+
+        for half in range(2):
+            view = sig[:, 4 * half : 4 * (half + 1), :].rearrange("p i n -> p (i n)")
+            nc.scalar.activation(out=view, in_=view, func=ACT.Ln, bias=LN_FLOOR)
+
+        def powers(k):
+            c, a = divmod(k, 2)
+            for t in range(4):
+                nc.scalar.activation(
+                    out=sp[k % 4][:, t, :],
+                    in_=sig[:, 4 * a + t, CHUNK * c : CHUNK * (c + 1)],
+                    func=ACT.Exp,
+                    scale=gam[:, t, a : a + 1],
+                )
+            for t in range(4):
+                nc.scalar.activation(
+                    out=sq[k % 4][:, t, :], in_=sp[k % 4][:, t, :], func=ACT.Square, scale=-1.0, bias=shift[:, t, a : a + 1]
+                )
+
+        def polys(k):
+            a = k % 2
+            for m, (src, mul, sub) in enumerate(((sp, slope1, off1), (sq, slope2, off2))):
+                for t in range(4):
+                    nc.vector.tensor_scalar(
+                        out=rp[k % 2][:, t, CHUNK * m : CHUNK * (m + 1)],
+                        in0=src[k % 4][:, t, :],
+                        scalar1=mul[:, t, a : a + 1],
+                        scalar2=sub[:, t, a : a + 1],
+                        op0=ALU.mult,
+                        op1=ALU.subtract,
+                    )
+
+        def r_group(k):
+            interleave(ri[k % 2][:], rp[k % 2][:])
+
+        def r_quant(k):
+            nc.vector.quantize_mx(out=rq[k % 3][:].bitcast(FP8X4), scales=rs[k % 3][:], in_=ri[k % 2][:])
+
+        def mix(k):
+            c, a = divmod(k, 2)
+            for m in range(2):
+                for jj in range(2):
+                    cols = slice(CHUNK * m + 128 * jj, CHUNK * m + 128 * (jj + 1))
+                    for oh in range(2):
+                        ocols = slice(512 * oh, 512 * (oh + 1))
+                        nc.tensor.matmul_mx(
+                            out=bank[4 * (c % 2) + 2 * jj + oh][:],
+                            lhsT=rq[k % 3][:, cols].bitcast(FP8X4),
+                            lhsT_scale=rs[k % 3][:, cols],
+                            rhs=w2q[2 * a + m][:, ocols].bitcast(FP8X4),
+                            rhs_scale=w2s[2 * a + m][:, ocols],
+                            start=(a == 0 and m == 0),
+                            stop=(a == 1 and m == 1),
+                        )
+
+        def drain(c, shared):
+            for b in range(4):
+                jj, oh = divmod(b, 2)
+                i = 4 * (c % 2) + b
+                if shared and b % 2 == 1:
+                    nc.vector.tensor_copy(out=ob[i][:], in_=bank[i][:])
+                else:
+                    nc.scalar.copy(out=ob[i][:], in_=bank[i][:])
+                nc.sync.dma_start(out=outv[2 * c + jj][:, 512 * oh : 512 * (oh + 1)], in_=ob[i][:])
+
+        powers(0)
+        powers(1)
+        polys(0)
+        w2_quant(7)
+        r_group(0)
+        drain_after = {3: 0, 6: 1, 7: 2}
+        for k in range(1, STEPS):
+            if k + 1 < STEPS:
+                powers(k + 1)
+            polys(k)
+            r_quant(k - 1)
+            mix(k - 1)
+            r_group(k)
+            if k + 1 in drain_after:
+                drain(drain_after[k + 1], False)
+        r_quant(STEPS - 1)
+        mix(STEPS - 1)
+        drain(3, True)

@@ -19,8 +19,11 @@ ALU = mybir.AluOpType
 
 P = 128
 TILES = 8
-CHUNK = 256
-STEPS = 8
+X_LOADS = [1, 1, 2, 2, 2]
+CHUNKS = [256,256,256,128,128]
+WIDE = max(CHUNKS)
+STEPS = 2 * len(CHUNKS)
+DRAINS = {3: [(0, True), (1, True), (2, True), (3, True)], 5: [(4, True), (5, True), (6, True), (7, True)], 7: [(8, True), (9, True)], 8: [(10, True), (11, True)], 9: [(12, True), (13, True)], 10: [(14, True), (15, False), (16, True), (17, False)]}
 LN_FLOOR = 2.0 ** -64
 
 
@@ -37,9 +40,9 @@ def tile_fractionaljacobikantwodegree_d1p_kernel(
 
         bank = [ps.tile([P, 512], F32, name="bank%d" % i) for i in range(8)]
 
-        xb = tiles("xbytes", 2, [P, 2 * D], U8) + tiles("xbytes_late", 1, [P, 4 * D], U8)
+        xb = [sb.tile([P, n * D], U8, name="xbytes%d" % i, align_bytes=64) for i, n in enumerate(X_LOADS)]
         xs = tiles("xscale", 1, [P, TILES * 8], F32)[0]
-        xw = tiles("xwide", 4, [P, D], BF16)
+        xw = tiles("xwide", TILES, [P, D], BF16)
         xg = tiles("xgrouped", 2, [P, 2, 2048], BF16)
         xq = tiles("xcodes", 2, [P, 2, 512], U32)
         xqs = tiles("xplane", 2, [P, 2, 512], U8)
@@ -58,12 +61,12 @@ def tile_fractionaljacobikantwodegree_d1p_kernel(
         w2i = tiles("w2grouped", 2, [P, 2048], BF16)
         w2q = tiles("w2codes", 4, [P, O], U32)
         w2s = tiles("w2plane", 4, [P, O], U8)
-        sp = tiles("spow", 4, [P, 4, CHUNK], F32)
-        sq = tiles("ssq", 4, [P, 4, CHUNK], F32)
-        rp = tiles("rplanar", 2, [P, 4, 2 * CHUNK], BF16)
-        ri = tiles("rgrouped", 2, [P, 2048], BF16)
-        rq = tiles("rcodes", 3, [P, 2 * CHUNK], U32)
-        rs = tiles("rplane", 3, [P, 2 * CHUNK], U8)
+        sp = tiles("spow", 4, [P, 4, WIDE], F32)
+        sq = tiles("ssq", 4, [P, 4, WIDE], F32)
+        rp = tiles("rplanar", 2, [P, 4, 2 * WIDE], BF16)
+        ri = tiles("rgrouped", 2, [P, 8 * WIDE], BF16)
+        rq = tiles("rcodes", 3, [P, 2 * WIDE], U32)
+        rs = tiles("rplane", 3, [P, 2 * WIDE], U8)
         ob = tiles("obuf", 8, [P, 512], F32)
 
         ctx.enter_context(tc.manual_schedule())
@@ -72,24 +75,40 @@ def tile_fractionaljacobikantwodegree_d1p_kernel(
         outv = out.rearrange("(p j) o -> j p o", j=TILES)
 
         def xbytes_of(j):
-            if j < 4:
-                return xb[j // 2][:, (j % 2) * D : (j % 2 + 1) * D]
-            return xb[2][:, (j - 4) * D : (j - 3) * D]
+            i = max(i for i in range(len(X_LOADS)) if sum(X_LOADS[:i]) <= j)
+            r = j - sum(X_LOADS[:i])
+            return xb[i][:, r * D : (r + 1) * D]
 
+        def load_x(i):
+            first = sum(X_LOADS[:i])
+            nc.sync.dma_start(out=xb[i][:], in_=xv[:, first * D : (first + X_LOADS[i]) * D])
+
+        nc.scalar.dma_start(out=xs[:], in_=x_scale.rearrange("(p j) b -> p (j b)", j=TILES))
         nc.vector.memset(warm[0][:], 0.0)
         nc.vector.memset(s1r[:].rearrange("p g n -> p (g n)").bitcast(I32), 0)
         nc.vector.memset(cperm[:], 0.0)
         nc.scalar.activation(out=warm[1][:], in_=warm[0][:], func=ACT.Sigmoid)
         make_identity(nc, ident[:])
 
-        nc.sync.dma_start(out=xs[:], in_=x_scale.rearrange("(p j) b -> p (j b)", j=TILES))
-        nc.sync.dma_start(out=xb[0][:, 0 : 2 * D], in_=xv[:, 0 : 2 * D])
-        nc.sync.dma_start(out=xb[1][:, 0 : 2 * D], in_=xv[:, 2 * D : 4 * D])
-        s1v = w1_scales.rearrange("g (a r) n -> r a g n", r=4)
-        for r in range(4):
-            nc.sync.dma_start(out=s1r[r:P:32].bitcast(I32), in_=s1v[r].bitcast(I32))
-        nc.sync.dma_start(out=w1r[:].bitcast(I32), in_=w1_words.rearrange("g p n -> p g n").bitcast(I32))
-        nc.sync.dma_start(out=xb[2][:], in_=xv[:, 4 * D : 8 * D])
+        def load_scales():
+            s1v = w1_scales.rearrange("g (a r) n -> r a g n", r=4)
+            for r in range(4):
+                nc.sync.dma_start(out=s1r[r:P:32].bitcast(I32), in_=s1v[r].bitcast(I32))
+
+        def load_w1(b):
+            cols = slice(1024 * b, 1024 * (b + 1))
+            nc.sync.dma_start(
+                out=w1r[:, :, cols].bitcast(I32), in_=w1_words.rearrange("g p n -> p g n")[:, :, cols].bitcast(I32)
+            )
+
+        load_x(0)
+        load_x(1)
+        load_x(2)
+        load_x(3)
+        load_x(4)
+        load_scales()
+        load_w1(0)
+        load_w1(1)
         nc.sync.dma_start(out=crow[0:2, :], in_=gamma.rearrange("(a n) -> a n", a=2))
         nc.sync.dma_start(out=crow[2:4, :], in_=alpha.rearrange("(a n) -> a n", a=2))
         nc.sync.dma_start(out=crow[4:6, :], in_=beta.rearrange("(a n) -> a n", a=2))
@@ -106,53 +125,55 @@ def tile_fractionaljacobikantwodegree_d1p_kernel(
                 cols = slice(128 * b, 128 * (b + 1))
                 sc = xs[:, 8 * j + b : 8 * j + b + 1]
                 if on_scalar:
-                    nc.scalar.activation(out=xw[j % 4][:, cols], in_=src[:, cols].bitcast(FP8), func=ACT.Copy, scale=sc)
+                    nc.scalar.activation(out=xw[j][:, cols], in_=src[:, cols].bitcast(FP8), func=ACT.Copy, scale=sc)
                 else:
                     nc.vector.tensor_scalar(
-                        out=xw[j % 4][:, cols], in0=src[:, cols].bitcast(FP8), scalar1=sc, scalar2=None, op0=ALU.mult
+                        out=xw[j][:, cols], in0=src[:, cols].bitcast(FP8), scalar1=sc, scalar2=None, op0=ALU.mult
                     )
 
         def turn(j):
-            words = xw[j % 4][:].bitcast(F32)
+            words = xw[j][:].bitcast(F32)
             for a in range(2):
                 for u in range(2):
                     i = 2 * a + u
                     nc.tensor.transpose(
-                        bank[j % 4][:, 128 * i : 128 * (i + 1)], words[:, 256 * a + u : 256 * (a + 1) : 2], ident[:]
+                        bank[j][:, 128 * i : 128 * (i + 1)], words[:, 256 * a + u : 256 * (a + 1) : 2], ident[:]
                     )
 
         def unload(j, on_scalar):
             dst = xg[j // 4][:].bitcast(F32)[:, :, 256 * (j % 4) : 256 * (j % 4 + 1)].rearrange("p a (r u) -> p a r u", u=2)
-            src = bank[j % 4][:].rearrange("p (a u r) -> p a r u", a=2, u=2)
+            src = bank[j][:].rearrange("p (a u r) -> p a r u", a=2, u=2)
             if on_scalar:
                 nc.scalar.copy(out=dst, in_=src)
             else:
                 nc.vector.tensor_copy(out=dst, in_=src)
 
-        def quant_x(pair):
-            h, c = divmod(pair, 2)
-            for a in range(2):
-                nc.vector.quantize_mx(
-                    out=xq[h][:, a, 256 * c : 256 * (c + 1)].bitcast(FP8X4),
-                    scales=xqs[h][:, a, 256 * c : 256 * (c + 1)],
-                    in_=xg[h][:, a, 1024 * c : 1024 * (c + 1)],
-                )
+        def quant_x(h, a):
+            nc.vector.quantize_mx(out=xq[h][:, a, :].bitcast(FP8X4), scales=xqs[h][:, a, :], in_=xg[h][:, a, :])
 
-        def permute_w1():
+        def permute_scales():
             for a in range(2):
                 nc.vector.tensor_copy(
                     out=s1p[:, a, :].bitcast(I32).rearrange("p (b t q) -> p b t q", b=2, t=4),
                     in_=s1r[:, a, :].bitcast(I32).rearrange("p (b q t) -> p b t q", b=2, t=4),
                 )
-                for b in range(2):
-                    cols = slice(1024 * b, 1024 * (b + 1))
-                    nc.vector.tensor_copy(
-                        out=w1p[:, a, cols].bitcast(I32).rearrange("p (t q w) -> p t q w", t=4, w=2),
-                        in_=w1r[:, a, cols].bitcast(I32).rearrange("p (q t w) -> p t q w", t=4, w=2),
-                    )
+
+        def permute_w1(b):
+            cols = slice(1024 * b, 1024 * (b + 1))
+            for a in range(2):
+                nc.vector.tensor_copy(
+                    out=w1p[:, a, cols].bitcast(I32).rearrange("p (t q w) -> p t q w", t=4, w=2),
+                    in_=w1r[:, a, cols].bitcast(I32).rearrange("p (q t w) -> p t q w", t=4, w=2),
+                )
+
+        def permute_rows():
+            nc.vector.tensor_copy(
+                out=cperm[0:10, :].rearrange("p (t q e) -> p t q e", t=4, e=4),
+                in_=crow[0:10, :].rearrange("p (q t e) -> p t q e", t=4, e=4),
+            )
 
         def project(h, i):
-            z = bank[4 + i % 4]
+            z = bank[i % 4]
             for a in range(2):
                 nc.tensor.matmul_mx(
                     out=z[:],
@@ -187,39 +208,46 @@ def tile_fractionaljacobikantwodegree_d1p_kernel(
         turn(2)
         unload(1, True)
         turn(3)
-        unload(2, True)
-        permute_w1()
-        quant_x(0)
-        unload(3, True)
         widen(4, False)
-        quant_x(1)
-        widen(5, True)
-        widen(6, False)
-        widen(7, False)
-        for i in range(4):
-            project(0, i)
+        unload(2, True)
+        widen(5, False)
         turn(4)
+        unload(3, True)
+        widen(6, True)
+        widen(7, False)
         turn(5)
+        permute_scales()
+        permute_w1(0)
+        quant_x(0, 0)
+        turn(7)
+        turn(6)
+        quant_x(0, 1)
+        project(0, 0)
+        permute_w1(1)
         unload(4, False)
         unload(5, False)
+        unload(7, False)
+        unload(6, False)
+        permute_rows()
+        quant_x(1, 0)
+        quant_x(1, 1)
+        project(0, 1)
+        project(0, 2)
+        project(0, 3)
         project(0, 4)
         project(0, 5)
-        turn(6)
-        turn(7)
-        unload(6, False)
-        quant_x(2)
-        unload(7, False)
-        nc.vector.tensor_copy(
-            out=cperm[0:10, :].rearrange("p (t q e) -> p t q e", t=4, e=4),
-            in_=crow[0:10, :].rearrange("p (q t e) -> p t q e", t=4, e=4),
-        )
-        quant_x(3)
         project(0, 6)
         project(0, 7)
+        project(1, 0)
+        project(1, 1)
+        project(1, 2)
+        project(1, 3)
+        project(1, 4)
+        project(1, 5)
+        project(1, 6)
+        project(1, 7)
         for t in range(4):
-            nc.tensor.transpose(bank[0][:, 128 * t : 128 * (t + 1)], cperm[:, 128 * t : 128 * (t + 1)], ident[:])
-        for i in range(TILES):
-            project(1, i)
+            nc.tensor.transpose(bank[7][:, 128 * t : 128 * (t + 1)], cperm[:, 128 * t : 128 * (t + 1)], ident[:])
 
         gam, al, be, g0, g1 = [coef[:, :, 2 * v : 2 * v + 2] for v in range(5)]
         ab, slope1, off1, ab4, inv, shift, c2h, slope2, eh, off2 = [c[:] for c in cw]
@@ -229,7 +257,7 @@ def tile_fractionaljacobikantwodegree_d1p_kernel(
 
         small = [
             lambda: nc.vector.tensor_copy(
-                out=coef[:], in_=bank[0][:].rearrange("p (t r) -> p t r", t=4)[:, :, 0:16]
+                out=coef[:], in_=bank[7][:].rearrange("p (t r) -> p t r", t=4)[:, :, 0:16]
             ),
             lambda: nc.vector.tensor_tensor(out=ab, in0=al, in1=be, op=ALU.add),
             lambda: stt(off1, be, 1.0, g0, ALU.add),
@@ -243,94 +271,115 @@ def tile_fractionaljacobikantwodegree_d1p_kernel(
             lambda: stt(off2, eh, 0.5, g1, ALU.mult),
         ]
         w2_group(0)
-        small[0]()
         for u in range(1, 8):
-            w2_group(u)
-            if u <= 5:
-                small[2 * u - 1]()
-            w2_quant(u - 1)
-            if u <= 5:
-                small[2 * u]()
+            for step in (lambda: w2_group(u), lambda: w2_quant(u - 1)):
+                step()
+                if u >= 3:
+                    for call in small[:1]:
+                        call()
+                    small = small[1:]
+        for call in small:
+            call()
+        w2_quant(7)
 
         for half in range(2):
             view = sig[:, 4 * half : 4 * (half + 1), :].rearrange("p i n -> p (i n)")
             nc.scalar.activation(out=view, in_=view, func=ACT.Ln, bias=LN_FLOOR)
 
-        def powers(k):
+        nb = len(sp)
+
+        def span(k):
             c, a = divmod(k, 2)
+            return sum(CHUNKS[:c]), CHUNKS[c], a
+
+        def powers(k):
+            first, n, a = span(k)
             for t in range(4):
                 nc.scalar.activation(
-                    out=sp[k % 4][:, t, :],
-                    in_=sig[:, 4 * a + t, CHUNK * c : CHUNK * (c + 1)],
-                    func=ACT.Exp,
-                    scale=gam[:, t, a : a + 1],
+                    out=sp[k % nb][:, t, 0:n], in_=sig[:, 4 * a + t, first : first + n], func=ACT.Exp, scale=gam[:, t, a : a + 1]
                 )
             for t in range(4):
                 nc.scalar.activation(
-                    out=sq[k % 4][:, t, :], in_=sp[k % 4][:, t, :], func=ACT.Square, scale=-1.0, bias=shift[:, t, a : a + 1]
+                    out=sq[k % nb][:, t, 0:n], in_=sp[k % nb][:, t, 0:n], func=ACT.Square, scale=-1.0, bias=shift[:, t, a : a + 1]
                 )
 
-        def polys(k):
-            a = k % 2
-            for m, (src, mul, sub) in enumerate(((sp, slope1, off1), (sq, slope2, off2))):
-                for t in range(4):
-                    nc.vector.tensor_scalar(
-                        out=rp[k % 2][:, t, CHUNK * m : CHUNK * (m + 1)],
-                        in0=src[k % 4][:, t, :],
-                        scalar1=mul[:, t, a : a + 1],
-                        scalar2=sub[:, t, a : a + 1],
-                        op0=ALU.mult,
-                        op1=ALU.subtract,
+        def poly(k, m):
+            first, n, a = span(k)
+            src, mul, sub = ((sp, slope1, off1), (sq, slope2, off2))[m]
+            for t in range(4):
+                nc.vector.tensor_scalar(
+                    out=rp[k % 2][:, t, n * m : n * (m + 1)],
+                    in0=src[k % nb][:, t, 0:n],
+                    scalar1=mul[:, t, a : a + 1],
+                    scalar2=sub[:, t, a : a + 1],
+                    op0=ALU.mult,
+                    op1=ALU.subtract,
+                )
+
+        def r_group(k, lo, hi):
+            n = span(k)[1]
+            interleave(ri[k % 2][:, 4 * n * lo : 4 * n * hi], rp[k % 2][:, :, n * lo : n * hi])
+
+        def r_quant(k, lo, hi):
+            n = span(k)[1]
+            nc.vector.quantize_mx(
+                out=rq[k % 3][:, n * lo : n * hi].bitcast(FP8X4),
+                scales=rs[k % 3][:, n * lo : n * hi],
+                in_=ri[k % 2][:, 4 * n * lo : 4 * n * hi],
+            )
+
+        pieces = [(j, 512 * oh, 512) for j in range(TILES - 1) for oh in range(2)]
+        pieces += [(TILES - 1, 256 * oq, 256) for oq in range(4)]
+
+        def mix(k, m):
+            first, n, a = span(k)
+            for i, (j, o0, width) in enumerate(pieces):
+                if first <= 128 * j < first + n:
+                    cols = slice(n * m + 128 * j - first, n * m + 128 * (j + 1) - first)
+                    nc.tensor.matmul_mx(
+                        out=bank[i % 8][:, 0:width],
+                        lhsT=rq[k % 3][:, cols].bitcast(FP8X4),
+                        lhsT_scale=rs[k % 3][:, cols],
+                        rhs=w2q[2 * a + m][:, o0 : o0 + width].bitcast(FP8X4),
+                        rhs_scale=w2s[2 * a + m][:, o0 : o0 + width],
+                        start=(a == 0 and m == 0),
+                        stop=(a == 1 and m == 1),
                     )
 
-        def r_group(k):
-            interleave(ri[k % 2][:], rp[k % 2][:])
+        def drain(i, on_scalar):
+            j, o0, width = pieces[i]
+            src, dst = bank[i % 8][:, 0:width], ob[i % 8][:, 0:width]
+            if on_scalar:
+                nc.scalar.copy(out=dst, in_=src)
+            else:
+                nc.vector.tensor_copy(out=dst, in_=src)
+            nc.sync.dma_start(out=outv[j][:, o0 : o0 + width], in_=dst)
 
-        def r_quant(k):
-            nc.vector.quantize_mx(out=rq[k % 3][:].bitcast(FP8X4), scales=rs[k % 3][:], in_=ri[k % 2][:])
-
-        def mix(k):
-            c, a = divmod(k, 2)
-            for m in range(2):
-                for jj in range(2):
-                    cols = slice(CHUNK * m + 128 * jj, CHUNK * m + 128 * (jj + 1))
-                    for oh in range(2):
-                        ocols = slice(512 * oh, 512 * (oh + 1))
-                        nc.tensor.matmul_mx(
-                            out=bank[4 * (c % 2) + 2 * jj + oh][:],
-                            lhsT=rq[k % 3][:, cols].bitcast(FP8X4),
-                            lhsT_scale=rs[k % 3][:, cols],
-                            rhs=w2q[2 * a + m][:, ocols].bitcast(FP8X4),
-                            rhs_scale=w2s[2 * a + m][:, ocols],
-                            start=(a == 0 and m == 0),
-                            stop=(a == 1 and m == 1),
-                        )
-
-        def drain(c, shared):
-            for b in range(4):
-                jj, oh = divmod(b, 2)
-                i = 4 * (c % 2) + b
-                if shared and b % 2 == 1:
-                    nc.vector.tensor_copy(out=ob[i][:], in_=bank[i][:])
-                else:
-                    nc.scalar.copy(out=ob[i][:], in_=bank[i][:])
-                nc.sync.dma_start(out=outv[2 * c + jj][:, 512 * oh : 512 * (oh + 1)], in_=ob[i][:])
-
+        last = STEPS - 1
         powers(0)
         powers(1)
-        polys(0)
-        w2_quant(7)
-        r_group(0)
-        drain_after = {3: 0, 6: 1, 7: 2}
+        poly(0, 0)
+        poly(0, 1)
+        r_group(0, 0, 2)
         for k in range(1, STEPS):
-            if k + 1 < STEPS:
+            if k < last:
                 powers(k + 1)
-            polys(k)
-            r_quant(k - 1)
-            mix(k - 1)
-            r_group(k)
-            if k + 1 in drain_after:
-                drain(drain_after[k + 1], False)
-        r_quant(STEPS - 1)
-        mix(STEPS - 1)
-        drain(3, True)
+            poly(k, 0)
+            if k == last:
+                r_quant(k - 1, 0, 2)
+                r_group(k, 0, 1)
+                poly(k, 1)
+                r_quant(k, 0, 1)
+            else:
+                poly(k, 1)
+                r_quant(k - 1, 0, 2)
+            mix(k - 1, 0)
+            mix(k - 1, 1)
+            r_group(k, k // last, 2)
+            for piece, on_scalar in DRAINS.get(k, ()):
+                drain(piece, on_scalar)
+        r_quant(last, 1, 2)
+        mix(last, 0)
+        mix(last, 1)
+        for piece, on_scalar in DRAINS[STEPS]:
+            drain(piece, on_scalar)

@@ -24,6 +24,7 @@ CHUNKS = [256,256,256,128,128]
 WIDE = max(CHUNKS)
 STEPS = 2 * len(CHUNKS)
 DRAINS = {3: [(0, True), (1, True), (2, True), (3, True)], 5: [(4, True), (5, True), (6, True), (7, True)], 7: [(8, True), (9, True)], 8: [(10, True), (11, True)], 9: [(12, True), (13, True)], 10: [(14, True), (15, False), (16, True), (17, False)]}
+SCALAR_WIDENS = (1, 6,)
 LN_FLOOR = 2.0 ** -64
 
 
@@ -56,6 +57,7 @@ def tile_fractionaljacobikantwodegree_d1p_kernel(
         coef = tiles("coef", 1, [P, 4, 16], F32)[0]
         cw = tiles("cwork", 10, [P, 4, 2], F32)
         warm = tiles("warm", 2, [P, 8], F32)
+        idle = tiles("idle", 1, [P, 512], BF16)[0]
         sig = tiles("sig", 1, [P, TILES, N], F32)[0]
         w2r = tiles("w2raw", 4, [P, 4, O], BF16)
         w2i = tiles("w2grouped", 2, [P, 2048], BF16)
@@ -84,6 +86,7 @@ def tile_fractionaljacobikantwodegree_d1p_kernel(
             nc.sync.dma_start(out=xb[i][:], in_=xv[:, first * D : (first + X_LOADS[i]) * D])
 
         nc.scalar.dma_start(out=xs[:], in_=x_scale.rearrange("(p j) b -> p (j b)", j=TILES))
+        nc.vector.memset(idle[:], 0.0)
         nc.vector.memset(warm[0][:], 0.0)
         nc.vector.memset(s1r[:].rearrange("p g n -> p (g n)").bitcast(I32), 0)
         nc.vector.memset(cperm[:], 0.0)
@@ -127,8 +130,13 @@ def tile_fractionaljacobikantwodegree_d1p_kernel(
                 if on_scalar:
                     nc.scalar.activation(out=xw[j][:, cols], in_=src[:, cols].bitcast(FP8), func=ACT.Copy, scale=sc)
                 else:
+                    halves = xw[j][:].rearrange("p (a u m e) -> p a m u e", a=2, u=2, e=2)
                     nc.vector.tensor_scalar(
-                        out=xw[j][:, cols], in0=src[:, cols].bitcast(FP8), scalar1=sc, scalar2=None, op0=ALU.mult
+                        out=halves[:, b // 4, 32 * (b % 4) : 32 * (b % 4 + 1)],
+                        in0=src[:, cols].bitcast(FP8).rearrange("p (m u e) -> p m u e", u=2, e=2),
+                        scalar1=sc,
+                        scalar2=None,
+                        op0=ALU.mult,
                     )
 
         def turn(j):
@@ -136,9 +144,14 @@ def tile_fractionaljacobikantwodegree_d1p_kernel(
             for a in range(2):
                 for u in range(2):
                     i = 2 * a + u
-                    nc.tensor.transpose(
-                        bank[j][:, 128 * i : 128 * (i + 1)], words[:, 256 * a + u : 256 * (a + 1) : 2], ident[:]
-                    )
+                    if j in SCALAR_WIDENS:
+                        picked = words[:, 256 * a + u : 256 * (a + 1) : 2]
+                    else:
+                        picked = words[:, 128 * i : 128 * (i + 1)]
+                    nc.tensor.transpose(bank[j][:, 128 * i : 128 * (i + 1)], picked, ident[:])
+
+        def keep_warm(j, width):
+            nc.tensor.matmul(bank[j][:, 0:width], lhsT=idle[:, 0:P], rhs=idle[:, 0:width], start=True, stop=True)
 
         def unload(j, on_scalar):
             dst = xg[j // 4][:].bitcast(F32)[:, :, 256 * (j % 4) : 256 * (j % 4 + 1)].rearrange("p a (r u) -> p a r u", u=2)
@@ -198,6 +211,8 @@ def tile_fractionaljacobikantwodegree_d1p_kernel(
             cols = slice(512 * (u % 2), 512 * (u % 2 + 1))
             nc.vector.quantize_mx(out=w2q[u // 2][:, cols].bitcast(FP8X4), scales=w2s[u // 2][:, cols], in_=w2i[u % 2][:])
 
+        for i in range(5):
+            keep_warm(0, 512)
         widen(0, False)
         widen(1, True)
         turn(0)
@@ -205,12 +220,14 @@ def tile_fractionaljacobikantwodegree_d1p_kernel(
         turn(1)
         unload(0, True)
         widen(3, False)
+        keep_warm(2, 512)
         turn(2)
         unload(1, True)
         turn(3)
         widen(4, False)
         unload(2, True)
         widen(5, False)
+        keep_warm(4, 512)
         turn(4)
         unload(3, True)
         widen(6, True)
@@ -219,6 +236,7 @@ def tile_fractionaljacobikantwodegree_d1p_kernel(
         permute_scales()
         permute_w1(0)
         quant_x(0, 0)
+        keep_warm(7, 512)
         turn(7)
         turn(6)
         quant_x(0, 1)

@@ -19,13 +19,24 @@ ALU = mybir.AluOpType
 
 P = 128
 TILES = 8
-X_LOADS = [1, 1, 2, 2, 2]
-CHUNKS = [256,256,256,128,128]
-WIDE = max(CHUNKS)
+BANK = 512
+RING = 4
+R_RING = 3
+
+X_LOADS = (1, 1, 1, 1, 2, 2)
+SCALAR_WIDENS = ((0, 0), (1, 0), (2, 0), (7, 0))
+SCALAR_UNLOADS = 6
+FIRST_WARM_UPS = 5
+WARM_BEFORE = (2, 4, 6)
+CHUNKS = (256, 256, 256, 128, 128)
 STEPS = 2 * len(CHUNKS)
-DRAINS = {3: [(0, True), (1, True), (2, True), (3, True)], 5: [(4, True), (5, True), (6, True), (7, True)], 7: [(8, True), (9, True)], 8: [(10, True), (11, True)], 9: [(12, True), (13, True)], 10: [(14, True), (15, False), (16, True), (17, False)]}
-SCALAR_WIDENS = (1, 6,)
-LN_FLOOR = 2.0 ** -64
+WIDE = max(CHUNKS)
+R1_ON_SCALAR = 4
+PIECES = [(j, BANK * h, BANK) for j in range(TILES - 1) for h in range(2)] + [
+    (TILES - 1, 256 * h, 256) for h in range(4)
+]
+DRAINS = {3: (0, 1, 2, 3), 5: (4, 5, 6, 7), 7: (8, 9), 8: (10, 11), 9: (12, 13)}
+CONSTANTS_FROM = 4
 
 
 def tile_fractionaljacobikantwodegree_d1p_kernel(
@@ -36,368 +47,361 @@ def tile_fractionaljacobikantwodegree_d1p_kernel(
         sb = ctx.enter_context(tc.tile_pool(name="sb", bufs=1))
         ps = ctx.enter_context(tc.psum_pool(name="ps", bufs=1))
 
+        def tile(name, shape, dtype):
+            return sb.tile(shape, dtype, name=name, align_bytes=64)
+
         def tiles(name, count, shape, dtype):
-            return [sb.tile(shape, dtype, name="%s%d" % (name, i), align_bytes=64) for i in range(count)]
+            return [tile("%s%d" % (name, i), shape, dtype) for i in range(count)]
 
-        bank = [ps.tile([P, 512], F32, name="bank%d" % i) for i in range(8)]
+        bank = [ps.tile([P, BANK], F32, name="bank%d" % i) for i in range(TILES)]
 
-        xb = [sb.tile([P, n * D], U8, name="xbytes%d" % i, align_bytes=64) for i, n in enumerate(X_LOADS)]
-        xs = tiles("xscale", 1, [P, TILES * 8], F32)[0]
-        xw = tiles("xwide", TILES, [P, D], BF16)
-        xg = tiles("xgrouped", 2, [P, 2, 2048], BF16)
-        xq = tiles("xcodes", 2, [P, 2, 512], U32)
-        xqs = tiles("xplane", 2, [P, 2, 512], U8)
-        w1r = tiles("w1raw", 1, [P, 2, 2 * H], U8)[0]
-        w1p = tiles("w1perm", 1, [P, 2, 2 * H], U8)[0]
-        s1r = tiles("s1raw", 1, [P, 2, H], U8)[0]
-        s1p = tiles("s1perm", 1, [P, 2, H], U8)[0]
-        ident = tiles("ident", 1, [P, P], F32)[0]
-        crow = tiles("crow", 1, [16, 512], BF16)[0]
-        cperm = tiles("cperm", 1, [P, 512], F32)[0]
-        coef = tiles("coef", 1, [P, 4, 16], F32)[0]
-        cw = tiles("cwork", 10, [P, 4, 2], F32)
-        warm = tiles("warm", 2, [P, 8], F32)
-        idle = tiles("idle", 1, [P, 512], BF16)[0]
-        sig = tiles("sig", 1, [P, TILES, N], F32)[0]
-        w2r = tiles("w2raw", 4, [P, 4, O], BF16)
-        w2i = tiles("w2grouped", 2, [P, 2048], BF16)
-        w2q = tiles("w2codes", 4, [P, O], U32)
-        w2s = tiles("w2plane", 4, [P, O], U8)
-        sp = tiles("spow", 4, [P, 4, WIDE], F32)
-        sq = tiles("ssq", 4, [P, 4, WIDE], F32)
-        rp = tiles("rplanar", 2, [P, 4, 2 * WIDE], BF16)
-        ri = tiles("rgrouped", 2, [P, 8 * WIDE], BF16)
-        rq = tiles("rcodes", 3, [P, 2 * WIDE], U32)
-        rs = tiles("rplane", 3, [P, 2 * WIDE], U8)
-        ob = tiles("obuf", 8, [P, 512], F32)
+        x_raw = [tile("x_raw%d" % i, [P, n * D], U8) for i, n in enumerate(X_LOADS)]
+        x_scales = tile("x_scales", [P, TILES * 8], F32)
+        x_wide = tiles("x_wide", TILES, [P, D], BF16)
+        x_grouped = tiles("x_grouped", 2, [P, 2, 4 * BANK], BF16)
+        x_codes = tiles("x_codes", 2, [P, 2, BANK], U32)
+        x_plane = tiles("x_plane", 2, [P, 2, BANK], U8)
+        w1_raw = tile("w1_raw", [P, 2, 2 * H], U8)
+        w1_codes = tile("w1_codes", [P, 2, 2 * H], U8)
+        w1_plane_raw = tile("w1_plane_raw", [P, 2, H], U8)
+        w1_plane = tile("w1_plane", [P, 2, H], U8)
+        ident = tile("ident", [P, P], F32)
+        rows_raw = tile("rows_raw", [16, BANK], BF16)
+        rows = tile("rows", [P, BANK], F32)
+        given = tile("given", [P, 4, 16], F32)
+        derived = tiles("derived", 15, [P, 4, 2], F32)
+        zero = tile("zero", [P, 1], F32)
+        one_half = tile("one_half", [P, 1], F32)
+        ln_floor = tile("ln_floor", [P, 1], F32)
+        idle = tile("idle", [P, BANK], BF16)
+        sig = tile("sig", [P, TILES, N], F32)
+        w2_raw = tiles("w2_raw", 4, [P, 4, O], BF16)
+        w2_grouped = tiles("w2_grouped", 2, [P, 4 * BANK], BF16)
+        w2_codes = tiles("w2_codes", 4, [P, O], U32)
+        w2_plane = tiles("w2_plane", 4, [P, O], U8)
+        power = tiles("power", RING, [P, 4, WIDE], F32)
+        square = tiles("square", RING, [P, 4, WIDE], F32)
+        r_flat = tiles("r_flat", R_RING, [P, 4, 2 * WIDE], BF16)
+        r_grouped = tiles("r_grouped", 2, [P, 8 * WIDE], BF16)
+        r_codes = tiles("r_codes", R_RING, [P, 2 * WIDE], U32)
+        r_plane = tiles("r_plane", R_RING, [P, 2 * WIDE], U8)
+        result = tiles("result", TILES, [P, BANK], F32)
 
         ctx.enter_context(tc.manual_schedule())
 
-        xv = x_bytes.rearrange("(p j) k -> p (j k)", j=TILES)
-        outv = out.rearrange("(p j) o -> j p o", j=TILES)
-
-        def xbytes_of(j):
-            i = max(i for i in range(len(X_LOADS)) if sum(X_LOADS[:i]) <= j)
-            r = j - sum(X_LOADS[:i])
-            return xb[i][:, r * D : (r + 1) * D]
-
-        def load_x(i):
-            first = sum(X_LOADS[:i])
-            nc.sync.dma_start(out=xb[i][:], in_=xv[:, first * D : (first + X_LOADS[i]) * D])
-
-        nc.scalar.dma_start(out=xs[:], in_=x_scale.rearrange("(p j) b -> p (j b)", j=TILES))
+        nc.scalar.dma_start(out=x_scales[:], in_=x_scale.rearrange("(p j) b -> p (j b)", j=TILES))
         nc.vector.memset(idle[:], 0.0)
-        nc.vector.memset(warm[0][:], 0.0)
-        nc.vector.memset(s1r[:].rearrange("p g n -> p (g n)").bitcast(I32), 0)
-        nc.vector.memset(cperm[:], 0.0)
-        nc.scalar.activation(out=warm[1][:], in_=warm[0][:], func=ACT.Sigmoid)
+        nc.vector.memset(zero[:], 0.0)
+        nc.vector.memset(w1_plane_raw[:].rearrange("p a n -> p (a n)").bitcast(I32), 0)
+        nc.vector.memset(rows[:], 0.0)
+        nc.scalar.activation(out=one_half[:], in_=zero[:], func=ACT.Sigmoid)
         make_identity(nc, ident[:])
 
-        def load_scales():
-            s1v = w1_scales.rearrange("g (a r) n -> r a g n", r=4)
-            for r in range(4):
-                nc.sync.dma_start(out=s1r[r:P:32].bitcast(I32), in_=s1v[r].bitcast(I32))
-
-        def load_w1(b):
-            cols = slice(1024 * b, 1024 * (b + 1))
+        x_view = x_bytes.rearrange("(p j) k -> p (j k)", j=TILES)
+        x_tile = []
+        for i, n in enumerate(X_LOADS):
+            first = len(x_tile)
+            nc.sync.dma_start(out=x_raw[i][:], in_=x_view[:, first * D : (first + n) * D])
+            x_tile.extend([x_raw[i][:, r * D : (r + 1) * D] for r in range(n)])
+        scale_rows = w1_scales.rearrange("a (c r) n -> r c a n", r=4)
+        for r in range(4):
+            nc.sync.dma_start(out=w1_plane_raw[r:P:32].bitcast(I32), in_=scale_rows[r].bitcast(I32))
+        for b in range(2):
+            cols = slice(H * b, H * (b + 1))
             nc.sync.dma_start(
-                out=w1r[:, :, cols].bitcast(I32), in_=w1_words.rearrange("g p n -> p g n")[:, :, cols].bitcast(I32)
+                out=w1_raw[:, :, cols].bitcast(I32), in_=w1_words.rearrange("a p n -> p a n")[:, :, cols].bitcast(I32)
             )
-
-        load_x(0)
-        load_x(1)
-        load_x(2)
-        load_x(3)
-        load_x(4)
-        load_scales()
-        load_w1(0)
-        load_w1(1)
-        nc.sync.dma_start(out=crow[0:2, :], in_=gamma.rearrange("(a n) -> a n", a=2))
-        nc.sync.dma_start(out=crow[2:4, :], in_=alpha.rearrange("(a n) -> a n", a=2))
-        nc.sync.dma_start(out=crow[4:6, :], in_=beta.rearrange("(a n) -> a n", a=2))
-        nc.sync.dma_start(out=crow[6:10, :], in_=g.rearrange("m (a n) -> (m a) n", a=2))
-        w2v = w2.rearrange("m (a q t e) o -> a m e q t o", a=2, t=4, e=4)
+        nc.sync.dma_start(out=rows_raw[0:2, :], in_=gamma.rearrange("(a n) -> a n", a=2))
+        nc.sync.dma_start(out=rows_raw[2:4, :], in_=alpha.rearrange("(a n) -> a n", a=2))
+        nc.sync.dma_start(out=rows_raw[4:6, :], in_=beta.rearrange("(a n) -> a n", a=2))
+        nc.sync.dma_start(out=rows_raw[6:10, :], in_=g.rearrange("m (a n) -> (m a) n", a=2))
+        w2_view = w2.rearrange("m (a q t e) o -> a m e q t o", a=2, t=4, e=4)
         for a in range(2):
             for m in range(2):
                 for e in range(4):
-                    nc.sync.dma_start(out=w2r[2 * a + m][e:P:4], in_=w2v[a, m, e])
+                    nc.sync.dma_start(out=w2_raw[2 * a + m][e:P:4], in_=w2_view[a, m, e])
 
-        def widen(j, on_scalar):
-            src = xbytes_of(j)
-            for b in range(8):
+        def widen(j, a):
+            for b in range(4 * a, 4 * a + 4):
                 cols = slice(128 * b, 128 * (b + 1))
-                sc = xs[:, 8 * j + b : 8 * j + b + 1]
-                if on_scalar:
-                    nc.scalar.activation(out=xw[j][:, cols], in_=src[:, cols].bitcast(FP8), func=ACT.Copy, scale=sc)
+                values = x_tile[j][:, cols].bitcast(FP8)
+                scale = x_scales[:, 8 * j + b : 8 * j + b + 1]
+                if (j, a) in SCALAR_WIDENS:
+                    nc.scalar.activation(out=x_wide[j][:, cols], in_=values, func=ACT.Copy, scale=scale)
                 else:
-                    halves = xw[j][:].rearrange("p (a u m e) -> p a m u e", a=2, u=2, e=2)
+                    split = x_wide[j][:].rearrange("p (a u m e) -> p a m u e", a=2, u=2, e=2)
                     nc.vector.tensor_scalar(
-                        out=halves[:, b // 4, 32 * (b % 4) : 32 * (b % 4 + 1)],
-                        in0=src[:, cols].bitcast(FP8).rearrange("p (m u e) -> p m u e", u=2, e=2),
-                        scalar1=sc,
+                        out=split[:, a, 32 * (b % 4) : 32 * (b % 4 + 1)],
+                        in0=values.rearrange("p (m u e) -> p m u e", u=2, e=2),
+                        scalar1=scale,
                         scalar2=None,
                         op0=ALU.mult,
                     )
 
         def turn(j):
-            words = xw[j][:].bitcast(F32)
+            words = x_wide[j][:].bitcast(F32)
             for a in range(2):
                 for u in range(2):
-                    i = 2 * a + u
-                    if j in SCALAR_WIDENS:
+                    cols = slice(128 * (2 * a + u), 128 * (2 * a + u + 1))
+                    if (j, a) in SCALAR_WIDENS:
                         picked = words[:, 256 * a + u : 256 * (a + 1) : 2]
                     else:
-                        picked = words[:, 128 * i : 128 * (i + 1)]
-                    nc.tensor.transpose(bank[j][:, 128 * i : 128 * (i + 1)], picked, ident[:])
+                        picked = words[:, cols]
+                    nc.tensor.transpose(bank[j][:, cols], picked, ident[:])
 
-        def keep_warm(j, width):
-            nc.tensor.matmul(bank[j][:, 0:width], lhsT=idle[:, 0:P], rhs=idle[:, 0:width], start=True, stop=True)
+        def warm_up(j):
+            nc.tensor.matmul(bank[j][:], lhsT=idle[:, 0:P], rhs=idle[:], start=True, stop=True)
 
-        def unload(j, on_scalar):
-            dst = xg[j // 4][:].bitcast(F32)[:, :, 256 * (j % 4) : 256 * (j % 4 + 1)].rearrange("p a (r u) -> p a r u", u=2)
-            src = bank[j][:].rearrange("p (a u r) -> p a r u", a=2, u=2)
-            if on_scalar:
+        def unload(j):
+            half, r = divmod(j, 4)
+            dst = x_grouped[half][:].bitcast(F32)[:, :, 256 * r : 256 * (r + 1)].rearrange("p a (c u) -> p a c u", u=2)
+            src = bank[j][:].rearrange("p (a u c) -> p a c u", a=2, u=2)
+            if j < SCALAR_UNLOADS:
                 nc.scalar.copy(out=dst, in_=src)
             else:
                 nc.vector.tensor_copy(out=dst, in_=src)
 
-        def quant_x(h, a):
-            nc.vector.quantize_mx(out=xq[h][:, a, :].bitcast(FP8X4), scales=xqs[h][:, a, :], in_=xg[h][:, a, :])
-
-        def permute_scales():
-            for a in range(2):
-                nc.vector.tensor_copy(
-                    out=s1p[:, a, :].bitcast(I32).rearrange("p (b t q) -> p b t q", b=2, t=4),
-                    in_=s1r[:, a, :].bitcast(I32).rearrange("p (b q t) -> p b t q", b=2, t=4),
-                )
-
-        def permute_w1(b):
-            cols = slice(1024 * b, 1024 * (b + 1))
-            for a in range(2):
-                nc.vector.tensor_copy(
-                    out=w1p[:, a, cols].bitcast(I32).rearrange("p (t q w) -> p t q w", t=4, w=2),
-                    in_=w1r[:, a, cols].bitcast(I32).rearrange("p (q t w) -> p t q w", t=4, w=2),
-                )
-
-        def permute_rows():
-            nc.vector.tensor_copy(
-                out=cperm[0:10, :].rearrange("p (t q e) -> p t q e", t=4, e=4),
-                in_=crow[0:10, :].rearrange("p (q t e) -> p t q e", t=4, e=4),
+        def quantise_x(half, a):
+            nc.vector.quantize_mx(
+                out=x_codes[half][:, a, :].bitcast(FP8X4), scales=x_plane[half][:, a, :], in_=x_grouped[half][:, a, :]
             )
 
-        def project(h, i):
+        def order_w1_plane():
+            for a in range(2):
+                nc.vector.tensor_copy(
+                    out=w1_plane[:, a, :].bitcast(I32).rearrange("p (b t q) -> p b t q", b=2, t=4),
+                    in_=w1_plane_raw[:, a, :].bitcast(I32).rearrange("p (b q t) -> p b t q", b=2, t=4),
+                )
+
+        def order_w1_codes(b):
+            cols = slice(H * b, H * (b + 1))
+            for a in range(2):
+                nc.vector.tensor_copy(
+                    out=w1_codes[:, a, cols].bitcast(I32).rearrange("p (t q w) -> p t q w", t=4, w=2),
+                    in_=w1_raw[:, a, cols].bitcast(I32).rearrange("p (q t w) -> p t q w", t=4, w=2),
+                )
+
+        def project(half, i):
             z = bank[i % 4]
             for a in range(2):
                 nc.tensor.matmul_mx(
                     out=z[:],
-                    lhsT=w1p[:, a, 256 * i : 256 * (i + 1)].bitcast(FP4X4),
-                    lhsT_scale=s1p[:, a, 128 * i : 128 * (i + 1)],
-                    rhs=xq[h][:, a, :].bitcast(FP8X4),
-                    rhs_scale=xqs[h][:, a, :],
+                    lhsT=w1_codes[:, a, 256 * i : 256 * (i + 1)].bitcast(FP4X4),
+                    lhsT_scale=w1_plane[:, a, 128 * i : 128 * (i + 1)],
+                    rhs=x_codes[half][:, a, :].bitcast(FP8X4),
+                    rhs_scale=x_plane[half][:, a, :],
                     start=(a == 0),
                     stop=(a == 1),
                 )
-            nc.scalar.activation(out=sig[:, i, 512 * h : 512 * (h + 1)], in_=z[:], func=ACT.Sigmoid)
+            nc.scalar.activation(out=sig[:, i, BANK * half : BANK * (half + 1)], in_=z[:], func=ACT.Sigmoid)
+
+        for i in range(FIRST_WARM_UPS):
+            warm_up(0)
+        for j in range(TILES - 1):
+            widen(j, 0)
+            widen(j, 1)
+            if j in WARM_BEFORE:
+                warm_up(j)
+            turn(j)
+            if 2 <= j < 6:
+                unload(j - 2)
+        widen(TILES - 1, 0)
+        order_w1_plane()
+        order_w1_codes(0)
+        widen(TILES - 1, 1)
+        quantise_x(0, 0)
+        turn(TILES - 1)
+        quantise_x(0, 1)
+        unload(4)
+        unload(5)
+        order_w1_codes(1)
+        unload(6)
+        unload(7)
+        nc.vector.tensor_copy(
+            out=rows[0:10, :].rearrange("p (t q e) -> p t q e", t=4, e=4),
+            in_=rows_raw[0:10, :].rearrange("p (q t e) -> p t q e", t=4, e=4),
+        )
+        quantise_x(1, 0)
+        quantise_x(1, 1)
+        nc.vector.tensor_scalar(out=ln_floor[:], in0=one_half[:], scalar1=2.0**-62, scalar2=None, op0=ALU.mult)
+        for half in range(2):
+            for i in range(TILES):
+                project(half, i)
+        for t in range(4):
+            nc.tensor.transpose(bank[7][:, 128 * t : 128 * (t + 1)], rows[:, 128 * t : 128 * (t + 1)], ident[:])
 
         def interleave(dst, src):
             nc.vector.tensor_copy(
                 out=dst.rearrange("p (c i t) -> p c t i", i=4, t=4), in_=src.rearrange("p t (c i) -> p c t i", i=4)
             )
 
-        def w2_group(u):
-            interleave(w2i[u % 2][:], w2r[u // 2][:, :, 512 * (u % 2) : 512 * (u % 2 + 1)])
+        def group_w2(n):
+            interleave(w2_grouped[n % 2][:], w2_raw[n // 2][:, :, BANK * (n % 2) : BANK * (n % 2 + 1)])
 
-        def w2_quant(u):
-            cols = slice(512 * (u % 2), 512 * (u % 2 + 1))
-            nc.vector.quantize_mx(out=w2q[u // 2][:, cols].bitcast(FP8X4), scales=w2s[u // 2][:, cols], in_=w2i[u % 2][:])
+        def quantise_w2(n):
+            cols = slice(BANK * (n % 2), BANK * (n % 2 + 1))
+            nc.vector.quantize_mx(
+                out=w2_codes[n // 2][:, cols].bitcast(FP8X4), scales=w2_plane[n // 2][:, cols], in_=w2_grouped[n % 2][:]
+            )
 
-        for i in range(5):
-            keep_warm(0, 512)
-        widen(0, False)
-        widen(1, True)
-        turn(0)
-        widen(2, False)
-        turn(1)
-        unload(0, True)
-        widen(3, False)
-        keep_warm(2, 512)
-        turn(2)
-        unload(1, True)
-        turn(3)
-        widen(4, False)
-        unload(2, True)
-        widen(5, False)
-        keep_warm(4, 512)
-        turn(4)
-        unload(3, True)
-        widen(6, True)
-        widen(7, False)
-        turn(5)
-        permute_scales()
-        permute_w1(0)
-        quant_x(0, 0)
-        keep_warm(7, 512)
-        turn(7)
-        turn(6)
-        quant_x(0, 1)
-        project(0, 0)
-        permute_w1(1)
-        unload(4, False)
-        unload(5, False)
-        unload(7, False)
-        unload(6, False)
-        permute_rows()
-        quant_x(1, 0)
-        quant_x(1, 1)
-        project(0, 1)
-        project(0, 2)
-        project(0, 3)
-        project(0, 4)
-        project(0, 5)
-        project(0, 6)
-        project(0, 7)
-        project(1, 0)
-        project(1, 1)
-        project(1, 2)
-        project(1, 3)
-        project(1, 4)
-        project(1, 5)
-        project(1, 6)
-        project(1, 7)
-        for t in range(4):
-            nc.tensor.transpose(bank[7][:, 128 * t : 128 * (t + 1)], cperm[:, 128 * t : 128 * (t + 1)], ident[:])
+        gam, al, be, g0, g1 = [given[:, :, 2 * v : 2 * v + 2] for v in range(5)]
+        ab, ab4, inv, c2_twice, minus_be1, al2_shift, shift_sq, lift = [d[:] for d in derived[0:8]]
+        slope1, base1, slope2, base2, shift, shift_twice, base2_open = [d[:] for d in derived[8:15]]
 
-        gam, al, be, g0, g1 = [coef[:, :, 2 * v : 2 * v + 2] for v in range(5)]
-        ab, slope1, off1, ab4, inv, shift, c2h, slope2, eh, off2 = [c[:] for c in cw]
+        def scaled(dst, a, number, b, op0):
+            nc.vector.scalar_tensor_tensor(out=dst, in0=a, scalar=number, in1=b, op0=op0, op1=ALU.mult)
 
-        def stt(o, a, s, b, op0):
-            nc.vector.scalar_tensor_tensor(out=o, in0=a, scalar=s, in1=b, op0=op0, op1=ALU.mult)
+        def affine(dst, a, mul, add):
+            nc.vector.tensor_scalar(out=dst, in0=a, scalar1=mul, scalar2=add, op0=ALU.mult, op1=ALU.add)
 
-        small = [
-            lambda: nc.vector.tensor_copy(
-                out=coef[:], in_=bank[7][:].rearrange("p (t r) -> p t r", t=4)[:, :, 0:16]
-            ),
+        constants = [
+            lambda: nc.vector.tensor_copy(out=given[:], in_=bank[7][:].rearrange("p (t r) -> p t r", t=4)[:, :, 0:16]),
             lambda: nc.vector.tensor_tensor(out=ab, in0=al, in1=be, op=ALU.add),
-            lambda: stt(off1, be, 1.0, g0, ALU.add),
-            lambda: nc.vector.tensor_scalar(out=ab4, in0=ab, scalar1=4.0, scalar2=None, op0=ALU.add),
-            lambda: stt(slope1, ab, 2.0, g0, ALU.add),
+            lambda: affine(minus_be1, be, -1.0, -1.0),
+            lambda: affine(ab4, ab, 1.0, 4.0),
+            lambda: scaled(slope1, ab, 2.0, g0, ALU.add),
             lambda: nc.vector.reciprocal(out=inv, in_=ab4),
-            lambda: stt(c2h, ab, 3.0, ab4, ALU.add),
-            lambda: stt(shift, be, 2.0, inv, ALU.add),
-            lambda: stt(slope2, c2h, 0.5, g1, ALU.mult),
-            lambda: stt(eh, al, 2.0, shift, ALU.add),
-            lambda: stt(off2, eh, 0.5, g1, ALU.mult),
+            lambda: scaled(c2_twice, ab, 3.0, ab4, ALU.add),
+            lambda: scaled(shift, be, 2.0, inv, ALU.add),
+            lambda: scaled(slope2, c2_twice, 0.5, g1, ALU.mult),
+            lambda: scaled(al2_shift, al, 2.0, shift, ALU.add),
+            lambda: scaled(shift_sq, shift, 1.0, shift, ALU.mult),
+            lambda: scaled(base2, al2_shift, -0.5, g1, ALU.mult),
+            lambda: scaled(lift, shift_sq, 1.0, slope2, ALU.mult),
+            lambda: scaled(base1, minus_be1, 1.0, g0, ALU.mult),
+            lambda: affine(shift_twice, shift, 2.0, 0.0),
+            lambda: nc.vector.tensor_tensor(out=base2_open, in0=lift, in1=base2, op=ALU.add),
         ]
-        w2_group(0)
-        for u in range(1, 8):
-            for step in (lambda: w2_group(u), lambda: w2_quant(u - 1)):
+        group_w2(0)
+        for n in range(1, 8):
+            for place, step in enumerate((lambda: group_w2(n), lambda: quantise_w2(n - 1))):
                 step()
-                if u >= 3:
-                    for call in small[:1]:
+                if n >= CONSTANTS_FROM:
+                    first = 4 * (n - CONSTANTS_FROM) + 2 * place
+                    for call in constants[first : first + 2]:
                         call()
-                    small = small[1:]
-        for call in small:
-            call()
-        w2_quant(7)
+        quantise_w2(7)
 
-        for half in range(2):
-            view = sig[:, 4 * half : 4 * (half + 1), :].rearrange("p i n -> p (i n)")
-            nc.scalar.activation(out=view, in_=view, func=ACT.Ln, bias=LN_FLOOR)
-
-        nb = len(sp)
+        for a in range(2):
+            view = sig[:, 4 * a : 4 * (a + 1), :].rearrange("p i n -> p (i n)")
+            nc.scalar.activation(out=view, in_=view, func=ACT.Ln, bias=ln_floor[:])
 
         def span(k):
             c, a = divmod(k, 2)
             return sum(CHUNKS[:c]), CHUNKS[c], a
 
+        def column(values, t, a):
+            return values[:, t, a : a + 1]
+
         def powers(k):
             first, n, a = span(k)
+            s = power[k % RING]
             for t in range(4):
                 nc.scalar.activation(
-                    out=sp[k % nb][:, t, 0:n], in_=sig[:, 4 * a + t, first : first + n], func=ACT.Exp, scale=gam[:, t, a : a + 1]
+                    out=s[:, t, 0:n], in_=sig[:, 4 * a + t, first : first + n], func=ACT.Exp, scale=column(gam, t, a)
                 )
-            for t in range(4):
-                nc.scalar.activation(
-                    out=sq[k % nb][:, t, 0:n], in_=sp[k % nb][:, t, 0:n], func=ACT.Square, scale=-1.0, bias=shift[:, t, a : a + 1]
-                )
-
-        def poly(k, m):
-            first, n, a = span(k)
-            src, mul, sub = ((sp, slope1, off1), (sq, slope2, off2))[m]
-            for t in range(4):
-                nc.vector.tensor_scalar(
-                    out=rp[k % 2][:, t, n * m : n * (m + 1)],
-                    in0=src[k % nb][:, t, 0:n],
-                    scalar1=mul[:, t, a : a + 1],
-                    scalar2=sub[:, t, a : a + 1],
-                    op0=ALU.mult,
-                    op1=ALU.subtract,
-                )
-
-        def r_group(k, lo, hi):
-            n = span(k)[1]
-            interleave(ri[k % 2][:, 4 * n * lo : 4 * n * hi], rp[k % 2][:, :, n * lo : n * hi])
-
-        def r_quant(k, lo, hi):
-            n = span(k)[1]
-            nc.vector.quantize_mx(
-                out=rq[k % 3][:, n * lo : n * hi].bitcast(FP8X4),
-                scales=rs[k % 3][:, n * lo : n * hi],
-                in_=ri[k % 2][:, 4 * n * lo : 4 * n * hi],
-            )
-
-        pieces = [(j, 512 * oh, 512) for j in range(TILES - 1) for oh in range(2)]
-        pieces += [(TILES - 1, 256 * oq, 256) for oq in range(4)]
-
-        def mix(k, m):
-            first, n, a = span(k)
-            for i, (j, o0, width) in enumerate(pieces):
-                if first <= 128 * j < first + n:
-                    cols = slice(n * m + 128 * j - first, n * m + 128 * (j + 1) - first)
-                    nc.tensor.matmul_mx(
-                        out=bank[i % 8][:, 0:width],
-                        lhsT=rq[k % 3][:, cols].bitcast(FP8X4),
-                        lhsT_scale=rs[k % 3][:, cols],
-                        rhs=w2q[2 * a + m][:, o0 : o0 + width].bitcast(FP8X4),
-                        rhs_scale=w2s[2 * a + m][:, o0 : o0 + width],
-                        start=(a == 0 and m == 0),
-                        stop=(a == 1 and m == 1),
+            if k == R1_ON_SCALAR:
+                for t in range(4):
+                    nc.scalar.activation(
+                        out=r_flat[k % R_RING][:, t, 0:n],
+                        in_=s[:, t, 0:n],
+                        func=ACT.Identity,
+                        scale=column(slope1, t, a),
+                        bias=column(base1, t, a),
+                    )
+            if k > 0:
+                for t in range(4):
+                    nc.scalar.activation(
+                        out=square[k % RING][:, t, 0:n],
+                        in_=s[:, t, 0:n],
+                        func=ACT.Square,
+                        scale=-1.0,
+                        bias=column(shift, t, a),
                     )
 
-        def drain(i, on_scalar):
-            j, o0, width = pieces[i]
-            src, dst = bank[i % 8][:, 0:width], ob[i % 8][:, 0:width]
-            if on_scalar:
-                nc.scalar.copy(out=dst, in_=src)
-            else:
-                nc.vector.tensor_copy(out=dst, in_=src)
-            nc.sync.dma_start(out=outv[j][:, o0 : o0 + width], in_=dst)
+        def form_r(k, m, t):
+            first, n, a = span(k)
+            src, slope, base = ((power, slope1, base1), (square, slope2, base2 if k > 0 else base2_open))[m]
+            affine(r_flat[k % R_RING][:, t, n * m : n * (m + 1)], src[k % RING][:, t, 0:n], column(slope, t, a), column(base, t, a))
+
+        def form_all(k, m):
+            if (k, m) != (R1_ON_SCALAR, 0):
+                for t in range(4):
+                    form_r(k, m, t)
+
+        def group_r(k, lo, hi):
+            n = span(k)[1]
+            interleave(r_grouped[k % 2][:, 4 * n * lo : 4 * n * hi], r_flat[k % R_RING][:, :, n * lo : n * hi])
+
+        def quantise_r(k, lo, hi):
+            n = span(k)[1]
+            nc.vector.quantize_mx(
+                out=r_codes[k % R_RING][:, n * lo : n * hi].bitcast(FP8X4),
+                scales=r_plane[k % R_RING][:, n * lo : n * hi],
+                in_=r_grouped[k % 2][:, 4 * n * lo : 4 * n * hi],
+            )
+
+        def mix(k):
+            first, n, a = span(k)
+            for m in range(2):
+                for i, (j, start, width) in enumerate(PIECES):
+                    if first <= 128 * j < first + n:
+                        cols = slice(n * m + 128 * j - first, n * m + 128 * (j + 1) - first)
+                        nc.tensor.matmul_mx(
+                            out=bank[i % TILES][:, 0:width],
+                            lhsT=r_codes[k % R_RING][:, cols].bitcast(FP8X4),
+                            lhsT_scale=r_plane[k % R_RING][:, cols],
+                            rhs=w2_codes[2 * a + m][:, start : start + width].bitcast(FP8X4),
+                            rhs_scale=w2_plane[2 * a + m][:, start : start + width],
+                            start=(a == 0 and m == 0),
+                            stop=(a == 1 and m == 1),
+                        )
+
+        out_view = out.rearrange("(p j) o -> j p o", j=TILES)
+
+        def drain(i, copy, queue):
+            j, start, width = PIECES[i]
+            dst = result[i % TILES][:, 0:width]
+            copy(out=dst, in_=bank[i % TILES][:, 0:width])
+            queue.dma_start(out=out_view[j][:, start : start + width], in_=dst)
 
         last = STEPS - 1
         powers(0)
         powers(1)
-        poly(0, 0)
-        poly(0, 1)
-        r_group(0, 0, 2)
-        for k in range(1, STEPS):
-            if k < last:
-                powers(k + 1)
-            poly(k, 0)
-            if k == last:
-                r_quant(k - 1, 0, 2)
-                r_group(k, 0, 1)
-                poly(k, 1)
-                r_quant(k, 0, 1)
-            else:
-                poly(k, 1)
-                r_quant(k - 1, 0, 2)
-            mix(k - 1, 0)
-            mix(k - 1, 1)
-            r_group(k, k // last, 2)
-            for piece, on_scalar in DRAINS.get(k, ()):
-                drain(piece, on_scalar)
-        r_quant(last, 1, 2)
-        mix(last, 0)
-        mix(last, 1)
-        for piece, on_scalar in DRAINS[STEPS]:
-            drain(piece, on_scalar)
+        for t in range(4):
+            s = power[0][:, t, 0 : CHUNKS[0]]
+            nc.vector.scalar_tensor_tensor(
+                out=square[0][:, t, 0 : CHUNKS[0]],
+                in0=s,
+                scalar=column(shift_twice, t, 0),
+                in1=s,
+                op0=ALU.subtract,
+                op1=ALU.mult,
+            )
+            form_r(0, 0, t)
+        form_all(0, 1)
+        group_r(0, 0, 1)
+        group_r(0, 1, 2)
+        for k in range(1, last):
+            powers(k + 1)
+            form_all(k, 0)
+            form_all(k, 1)
+            quantise_r(k - 1, 0, 2)
+            mix(k - 1)
+            group_r(k, 0, 2)
+            for i in DRAINS.get(k, ()):
+                drain(i, nc.scalar.copy, nc.sync)
+        form_all(last, 0)
+        quantise_r(last - 1, 0, 2)
+        group_r(last, 0, 1)
+        form_all(last, 1)
+        quantise_r(last, 0, 1)
+        mix(last - 1)
+        group_r(last, 1, 2)
+        for i in DRAINS[last]:
+            drain(i, nc.scalar.copy, nc.sync)
+        quantise_r(last, 1, 2)
+        mix(last)
+        for i in range(len(PIECES) - 4, len(PIECES), 2):
+            drain(i, nc.vector.tensor_copy, nc.sync)
+            drain(i + 1, nc.scalar.copy, nc.scalar)

from contextlib import ExitStack

import concourse.mybir as mybir
from concourse.masks import make_identity

N, D, H, O = 1024, 1024, 1024, 1024
FLOPS = 2 * N * D * H + 2 * 2 * N * H * O

F32 = mybir.dt.float32
BF16 = mybir.dt.bfloat16
I32 = mybir.dt.int32
U32 = mybir.dt.uint32
U8 = mybir.dt.uint8
FP8 = mybir.dt.float8_e4m3fn
FP8X4 = mybir.dt.float8_e4m3fn_x4
FP4X4 = mybir.dt.float4_e2m1fn_x4
ACT = mybir.ActivationFunctionType
ALU = mybir.AluOpType

P = 128
TILES = 8
BANK = 512
RING = 4
R_RING = 3

X_LOADS = (1, 1, 1, 1, 2, 2)
SCALAR_WIDENS = ((0, 0), (1, 0), (2, 0), (7, 0))
SCALAR_UNLOADS = 6
FIRST_WARM_UPS = 5
WARM_BEFORE = (2, 4, 6)
CHUNKS = (256, 256, 256, 128, 128)
STEPS = 2 * len(CHUNKS)
WIDE = max(CHUNKS)
R1_ON_SCALAR = 4
PIECES = [(j, BANK * h, BANK) for j in range(TILES - 1) for h in range(2)] + [
    (TILES - 1, 256 * h, 256) for h in range(4)
]
DRAINS = {3: (0, 1, 2, 3), 5: (4, 5, 6, 7), 7: (8, 9), 8: (10, 11), 9: (12, 13)}
CONSTANTS_FROM = 4


def tile_fractionaljacobikantwodegree_d1p_kernel(
    tc, x_bytes, x_scale, w1_words, w1_scales, gamma, alpha, beta, g, w2, out
):
    nc = tc.nc
    with ExitStack() as ctx:
        sb = ctx.enter_context(tc.tile_pool(name="sb", bufs=1))
        ps = ctx.enter_context(tc.psum_pool(name="ps", bufs=1))

        def tile(name, shape, dtype):
            return sb.tile(shape, dtype, name=name, align_bytes=64)

        def tiles(name, count, shape, dtype):
            return [tile("%s%d" % (name, i), shape, dtype) for i in range(count)]

        bank = [ps.tile([P, BANK], F32, name="bank%d" % i) for i in range(TILES)]

        x_raw = [tile("x_raw%d" % i, [P, n * D], U8) for i, n in enumerate(X_LOADS)]
        x_scales = tile("x_scales", [P, TILES * 8], F32)
        x_wide = tiles("x_wide", TILES, [P, D], BF16)
        x_grouped = tiles("x_grouped", 2, [P, 2, 4 * BANK], BF16)
        x_codes = tiles("x_codes", 2, [P, 2, BANK], U32)
        x_plane = tiles("x_plane", 2, [P, 2, BANK], U8)
        w1_raw = tile("w1_raw", [P, 2, 2 * H], U8)
        w1_codes = tile("w1_codes", [P, 2, 2 * H], U8)
        w1_plane_raw = tile("w1_plane_raw", [P, 2, H], U8)
        w1_plane = tile("w1_plane", [P, 2, H], U8)
        ident = tile("ident", [P, P], F32)
        rows_raw = tile("rows_raw", [16, BANK], BF16)
        rows = tile("rows", [P, BANK], F32)
        given = tile("given", [P, 4, 16], F32)
        derived = tiles("derived", 15, [P, 4, 2], F32)
        zero = tile("zero", [P, 1], F32)
        one_half = tile("one_half", [P, 1], F32)
        ln_floor = tile("ln_floor", [P, 1], F32)
        idle = tile("idle", [P, BANK], BF16)
        sig = tile("sig", [P, TILES, N], F32)
        w2_raw = tiles("w2_raw", 4, [P, 4, O], BF16)
        w2_grouped = tiles("w2_grouped", 2, [P, 4 * BANK], BF16)
        w2_codes = tiles("w2_codes", 4, [P, O], U32)
        w2_plane = tiles("w2_plane", 4, [P, O], U8)
        power = tiles("power", RING, [P, 4, WIDE], F32)
        square = tiles("square", RING, [P, 4, WIDE], F32)
        r_flat = tiles("r_flat", R_RING, [P, 4, 2 * WIDE], BF16)
        r_grouped = tiles("r_grouped", 2, [P, 8 * WIDE], BF16)
        r_codes = tiles("r_codes", R_RING, [P, 2 * WIDE], U32)
        r_plane = tiles("r_plane", R_RING, [P, 2 * WIDE], U8)
        result = tiles("result", TILES, [P, BANK], F32)

        ctx.enter_context(tc.manual_schedule())

        nc.scalar.dma_start(out=x_scales[:], in_=x_scale.rearrange("(p j) b -> p (j b)", j=TILES))
        nc.vector.memset(idle[:], 0.0)
        nc.vector.memset(zero[:], 0.0)
        nc.vector.memset(w1_plane_raw[:].rearrange("p a n -> p (a n)").bitcast(I32), 0)
        nc.vector.memset(rows[:], 0.0)
        nc.scalar.activation(out=one_half[:], in_=zero[:], func=ACT.Sigmoid)
        make_identity(nc, ident[:])

        x_view = x_bytes.rearrange("(p j) k -> p (j k)", j=TILES)
        x_tile = []
        for i, n in enumerate(X_LOADS):
            first = len(x_tile)
            nc.sync.dma_start(out=x_raw[i][:], in_=x_view[:, first * D : (first + n) * D])
            x_tile.extend([x_raw[i][:, r * D : (r + 1) * D] for r in range(n)])
        scale_rows = w1_scales.rearrange("a (c r) n -> r c a n", r=4)
        for r in range(4):
            nc.sync.dma_start(out=w1_plane_raw[r:P:32].bitcast(I32), in_=scale_rows[r].bitcast(I32))
        for b in range(2):
            cols = slice(H * b, H * (b + 1))
            nc.sync.dma_start(
                out=w1_raw[:, :, cols].bitcast(I32), in_=w1_words.rearrange("a p n -> p a n")[:, :, cols].bitcast(I32)
            )
        nc.sync.dma_start(out=rows_raw[0:2, :], in_=gamma.rearrange("(a n) -> a n", a=2))
        nc.sync.dma_start(out=rows_raw[2:4, :], in_=alpha.rearrange("(a n) -> a n", a=2))
        nc.sync.dma_start(out=rows_raw[4:6, :], in_=beta.rearrange("(a n) -> a n", a=2))
        nc.sync.dma_start(out=rows_raw[6:10, :], in_=g.rearrange("m (a n) -> (m a) n", a=2))
        w2_view = w2.rearrange("m (a q t e) o -> a m e q t o", a=2, t=4, e=4)
        for a in range(2):
            for m in range(2):
                for e in range(4):
                    nc.sync.dma_start(out=w2_raw[2 * a + m][e:P:4], in_=w2_view[a, m, e])

        def widen(j, a):
            for b in range(4 * a, 4 * a + 4):
                cols = slice(128 * b, 128 * (b + 1))
                values = x_tile[j][:, cols].bitcast(FP8)
                scale = x_scales[:, 8 * j + b : 8 * j + b + 1]
                if (j, a) in SCALAR_WIDENS:
                    nc.scalar.activation(out=x_wide[j][:, cols], in_=values, func=ACT.Copy, scale=scale)
                else:
                    split = x_wide[j][:].rearrange("p (a u m e) -> p a m u e", a=2, u=2, e=2)
                    nc.vector.tensor_scalar(
                        out=split[:, a, 32 * (b % 4) : 32 * (b % 4 + 1)],
                        in0=values.rearrange("p (m u e) -> p m u e", u=2, e=2),
                        scalar1=scale,
                        scalar2=None,
                        op0=ALU.mult,
                    )

        def turn(j):
            words = x_wide[j][:].bitcast(F32)
            for a in range(2):
                for u in range(2):
                    cols = slice(128 * (2 * a + u), 128 * (2 * a + u + 1))
                    if (j, a) in SCALAR_WIDENS:
                        picked = words[:, 256 * a + u : 256 * (a + 1) : 2]
                    else:
                        picked = words[:, cols]
                    nc.tensor.transpose(bank[j][:, cols], picked, ident[:])

        def warm_up(j):
            nc.tensor.matmul(bank[j][:], lhsT=idle[:, 0:P], rhs=idle[:], start=True, stop=True)

        def unload(j):
            half, r = divmod(j, 4)
            dst = x_grouped[half][:].bitcast(F32)[:, :, 256 * r : 256 * (r + 1)].rearrange("p a (c u) -> p a c u", u=2)
            src = bank[j][:].rearrange("p (a u c) -> p a c u", a=2, u=2)
            if j < SCALAR_UNLOADS:
                nc.scalar.copy(out=dst, in_=src)
            else:
                nc.vector.tensor_copy(out=dst, in_=src)

        def quantise_x(half, a):
            nc.vector.quantize_mx(
                out=x_codes[half][:, a, :].bitcast(FP8X4), scales=x_plane[half][:, a, :], in_=x_grouped[half][:, a, :]
            )

        def order_w1_plane():
            for a in range(2):
                nc.vector.tensor_copy(
                    out=w1_plane[:, a, :].bitcast(I32).rearrange("p (b t q) -> p b t q", b=2, t=4),
                    in_=w1_plane_raw[:, a, :].bitcast(I32).rearrange("p (b q t) -> p b t q", b=2, t=4),
                )

        def order_w1_codes(b):
            cols = slice(H * b, H * (b + 1))
            for a in range(2):
                nc.vector.tensor_copy(
                    out=w1_codes[:, a, cols].bitcast(I32).rearrange("p (t q w) -> p t q w", t=4, w=2),
                    in_=w1_raw[:, a, cols].bitcast(I32).rearrange("p (q t w) -> p t q w", t=4, w=2),
                )

        def project(half, i):
            z = bank[i % 4]
            for a in range(2):
                nc.tensor.matmul_mx(
                    out=z[:],
                    lhsT=w1_codes[:, a, 256 * i : 256 * (i + 1)].bitcast(FP4X4),
                    lhsT_scale=w1_plane[:, a, 128 * i : 128 * (i + 1)],
                    rhs=x_codes[half][:, a, :].bitcast(FP8X4),
                    rhs_scale=x_plane[half][:, a, :],
                    start=(a == 0),
                    stop=(a == 1),
                )
            nc.scalar.activation(out=sig[:, i, BANK * half : BANK * (half + 1)], in_=z[:], func=ACT.Sigmoid)

        for i in range(FIRST_WARM_UPS):
            warm_up(0)
        for j in range(TILES - 1):
            widen(j, 0)
            widen(j, 1)
            if j in WARM_BEFORE:
                warm_up(j)
            turn(j)
            if 2 <= j < 6:
                unload(j - 2)
        widen(TILES - 1, 0)
        order_w1_plane()
        order_w1_codes(0)
        widen(TILES - 1, 1)
        quantise_x(0, 0)
        turn(TILES - 1)
        quantise_x(0, 1)
        unload(4)
        unload(5)
        order_w1_codes(1)
        unload(6)
        unload(7)
        nc.vector.tensor_copy(
            out=rows[0:10, :].rearrange("p (t q e) -> p t q e", t=4, e=4),
            in_=rows_raw[0:10, :].rearrange("p (q t e) -> p t q e", t=4, e=4),
        )
        quantise_x(1, 0)
        quantise_x(1, 1)
        nc.vector.tensor_scalar(out=ln_floor[:], in0=one_half[:], scalar1=2.0**-62, scalar2=None, op0=ALU.mult)
        for half in range(2):
            for i in range(TILES):
                project(half, i)
        for t in range(4):
            nc.tensor.transpose(bank[7][:, 128 * t : 128 * (t + 1)], rows[:, 128 * t : 128 * (t + 1)], ident[:])

        def interleave(dst, src):
            nc.vector.tensor_copy(
                out=dst.rearrange("p (c i t) -> p c t i", i=4, t=4), in_=src.rearrange("p t (c i) -> p c t i", i=4)
            )

        def group_w2(n):
            interleave(w2_grouped[n % 2][:], w2_raw[n // 2][:, :, BANK * (n % 2) : BANK * (n % 2 + 1)])

        def quantise_w2(n):
            cols = slice(BANK * (n % 2), BANK * (n % 2 + 1))
            nc.vector.quantize_mx(
                out=w2_codes[n // 2][:, cols].bitcast(FP8X4), scales=w2_plane[n // 2][:, cols], in_=w2_grouped[n % 2][:]
            )

        gam, al, be, g0, g1 = [given[:, :, 2 * v : 2 * v + 2] for v in range(5)]
        ab, ab4, inv, c2_twice, minus_be1, al2_shift, shift_sq, lift = [d[:] for d in derived[0:8]]
        slope1, base1, slope2, base2, shift, shift_twice, base2_open = [d[:] for d in derived[8:15]]

        def scaled(dst, a, number, b, op0):
            nc.vector.scalar_tensor_tensor(out=dst, in0=a, scalar=number, in1=b, op0=op0, op1=ALU.mult)

        def affine(dst, a, mul, add):
            nc.vector.tensor_scalar(out=dst, in0=a, scalar1=mul, scalar2=add, op0=ALU.mult, op1=ALU.add)

        constants = [
            lambda: nc.vector.tensor_copy(out=given[:], in_=bank[7][:].rearrange("p (t r) -> p t r", t=4)[:, :, 0:16]),
            lambda: nc.vector.tensor_tensor(out=ab, in0=al, in1=be, op=ALU.add),
            lambda: affine(minus_be1, be, -1.0, -1.0),
            lambda: affine(ab4, ab, 1.0, 4.0),
            lambda: scaled(slope1, ab, 2.0, g0, ALU.add),
            lambda: nc.vector.reciprocal(out=inv, in_=ab4),
            lambda: scaled(c2_twice, ab, 3.0, ab4, ALU.add),
            lambda: scaled(shift, be, 2.0, inv, ALU.add),
            lambda: scaled(slope2, c2_twice, 0.5, g1, ALU.mult),
            lambda: scaled(al2_shift, al, 2.0, shift, ALU.add),
            lambda: scaled(shift_sq, shift, 1.0, shift, ALU.mult),
            lambda: scaled(base2, al2_shift, -0.5, g1, ALU.mult),
            lambda: scaled(lift, shift_sq, 1.0, slope2, ALU.mult),
            lambda: scaled(base1, minus_be1, 1.0, g0, ALU.mult),
            lambda: affine(shift_twice, shift, 2.0, 0.0),
            lambda: nc.vector.tensor_tensor(out=base2_open, in0=lift, in1=base2, op=ALU.add),
        ]
        group_w2(0)
        for n in range(1, 8):
            for place, step in enumerate((lambda: group_w2(n), lambda: quantise_w2(n - 1))):
                step()
                if n >= CONSTANTS_FROM:
                    first = 4 * (n - CONSTANTS_FROM) + 2 * place
                    for call in constants[first : first + 2]:
                        call()
        quantise_w2(7)

        for a in range(2):
            view = sig[:, 4 * a : 4 * (a + 1), :].rearrange("p i n -> p (i n)")
            nc.scalar.activation(out=view, in_=view, func=ACT.Ln, bias=ln_floor[:])

        def span(k):
            c, a = divmod(k, 2)
            return sum(CHUNKS[:c]), CHUNKS[c], a

        def column(values, t, a):
            return values[:, t, a : a + 1]

        def powers(k):
            first, n, a = span(k)
            s = power[k % RING]
            for t in range(4):
                nc.scalar.activation(
                    out=s[:, t, 0:n], in_=sig[:, 4 * a + t, first : first + n], func=ACT.Exp, scale=column(gam, t, a)
                )
            if k == R1_ON_SCALAR:
                for t in range(4):
                    nc.scalar.activation(
                        out=r_flat[k % R_RING][:, t, 0:n],
                        in_=s[:, t, 0:n],
                        func=ACT.Identity,
                        scale=column(slope1, t, a),
                        bias=column(base1, t, a),
                    )
            if k > 0:
                for t in range(4):
                    nc.scalar.activation(
                        out=square[k % RING][:, t, 0:n],
                        in_=s[:, t, 0:n],
                        func=ACT.Square,
                        scale=-1.0,
                        bias=column(shift, t, a),
                    )

        def form_r(k, m, t):
            first, n, a = span(k)
            src, slope, base = ((power, slope1, base1), (square, slope2, base2 if k > 0 else base2_open))[m]
            affine(r_flat[k % R_RING][:, t, n * m : n * (m + 1)], src[k % RING][:, t, 0:n], column(slope, t, a), column(base, t, a))

        def form_all(k, m):
            if (k, m) != (R1_ON_SCALAR, 0):
                for t in range(4):
                    form_r(k, m, t)

        def group_r(k, lo, hi):
            n = span(k)[1]
            interleave(r_grouped[k % 2][:, 4 * n * lo : 4 * n * hi], r_flat[k % R_RING][:, :, n * lo : n * hi])

        def quantise_r(k, lo, hi):
            n = span(k)[1]
            nc.vector.quantize_mx(
                out=r_codes[k % R_RING][:, n * lo : n * hi].bitcast(FP8X4),
                scales=r_plane[k % R_RING][:, n * lo : n * hi],
                in_=r_grouped[k % 2][:, 4 * n * lo : 4 * n * hi],
            )

        def mix(k):
            first, n, a = span(k)
            for m in range(2):
                for i, (j, start, width) in enumerate(PIECES):
                    if first <= 128 * j < first + n:
                        cols = slice(n * m + 128 * j - first, n * m + 128 * (j + 1) - first)
                        nc.tensor.matmul_mx(
                            out=bank[i % TILES][:, 0:width],
                            lhsT=r_codes[k % R_RING][:, cols].bitcast(FP8X4),
                            lhsT_scale=r_plane[k % R_RING][:, cols],
                            rhs=w2_codes[2 * a + m][:, start : start + width].bitcast(FP8X4),
                            rhs_scale=w2_plane[2 * a + m][:, start : start + width],
                            start=(a == 0 and m == 0),
                            stop=(a == 1 and m == 1),
                        )

        out_view = out.rearrange("(p j) o -> j p o", j=TILES)

        def drain(i, copy, queue):
            j, start, width = PIECES[i]
            dst = result[i % TILES][:, 0:width]
            copy(out=dst, in_=bank[i % TILES][:, 0:width])
            queue.dma_start(out=out_view[j][:, start : start + width], in_=dst)

        last = STEPS - 1
        powers(0)
        powers(1)
        for t in range(4):
            s = power[0][:, t, 0 : CHUNKS[0]]
            nc.vector.scalar_tensor_tensor(
                out=square[0][:, t, 0 : CHUNKS[0]],
                in0=s,
                scalar=column(shift_twice, t, 0),
                in1=s,
                op0=ALU.subtract,
                op1=ALU.mult,
            )
            form_r(0, 0, t)
        form_all(0, 1)
        group_r(0, 0, 1)
        group_r(0, 1, 2)
        for k in range(1, last):
            powers(k + 1)
            form_all(k, 0)
            form_all(k, 1)
            quantise_r(k - 1, 0, 2)
            mix(k - 1)
            group_r(k, 0, 2)
            for i in DRAINS.get(k, ()):
                drain(i, nc.scalar.copy, nc.sync)
        form_all(last, 0)
        quantise_r(last - 1, 0, 2)
        group_r(last, 0, 1)
        form_all(last, 1)
        quantise_r(last, 0, 1)
        mix(last - 1)
        group_r(last, 1, 2)
        for i in DRAINS[last]:
            drain(i, nc.scalar.copy, nc.sync)
        quantise_r(last, 1, 2)
        mix(last)
        for i in range(len(PIECES) - 4, len(PIECES), 2):
            drain(i, nc.vector.tensor_copy, nc.sync)
            drain(i + 1, nc.scalar.copy, nc.scalar)
